import numpy as np, ml_dtypes
CORES = [3,11,19,27,35,43,51,59]
N = 8
import mx_ref
BF = ml_dtypes.bfloat16
def gcols(t, e):
    v = np.concatenate([t.reshape(8, 16, -1, 4), np.zeros((8, 16, 1, 4), BF)], axis=2)
    return np.ascontiguousarray(np.stack([v[g][:, e[g]] for g in range(8)])).reshape(128, -1)
def tile(rs):
    return np.stack(rs, axis=2).reshape(128, -1).astype(BF)
def pick(q, e):
    c = np.concatenate([q[0].reshape(128, -1, 4), np.zeros((128, 1, 4), np.uint8)], axis=1); s = np.concatenate([q[1], np.ones((16, 1), np.uint8)], axis=1)
    return (np.ascontiguousarray(c[:, e].reshape(128, -1)), np.ascontiguousarray(s[:, e]))
def join(*qs):
    return (np.concatenate([q[0] for q in qs], axis=1), np.concatenate([q[1] for q in qs], axis=1))
def put(q, e, v):
    c, s = q[0].reshape(128, -1, 4).copy(), q[1].copy(); c[:, e] = v[0].reshape(128, -1, 4); s[:, e] = v[1]
    return (c.reshape(128, -1), s)
def pk(c, s):
    return (np.ascontiguousarray(c), mx_ref.live(s))
def emit(q):
    return q[0], q[1]
def packed(v, rng):
    q = [mx_ref.quantize(np.ascontiguousarray(v[r])) for r in range(N)]
    return np.stack([a for a, b in q]), np.stack([mx_ref.plane(b, rng) for a, b in q])
def values_of_codes():
    e, c = np.zeros((128, 128, 4), np.float32), np.zeros((128, 2, 4), np.uint8)
    e[np.arange(128), np.arange(128), 0] = 1
    c[:127, :, 0] = np.arange(256).reshape(2, 128).T[:127]
    return mx_ref.matmul(mx_ref.quantize(e.reshape(128, 512).astype(BF)), (c.reshape(128, 8), np.full((16, 2), 127, np.uint8))).T.reshape(-1).astype(np.float64)
CODE_VALUE, SCALE_VALUE = values_of_codes(), 2.0 ** (np.arange(256) - 127.0)
def decode(q):
    return (CODE_VALUE[q[0]].reshape(16, 8, -1, 4) * SCALE_VALUE[q[1]][:, None, :, None] + 0.0).reshape(128, -1).astype(np.float32)
def f(rng, *shape):
    return mx_ref.flush((rng.standard_normal(shape, dtype=np.float32) * np.exp2(rng.integers(-2, 3, shape[:-1] + (1,)))).astype(BF))
def wide(rng, *shape, cols=0):
    v = rng.standard_normal(shape, dtype=np.float32) * np.exp2(rng.integers(-12, 13, shape)).astype(np.float32)
    if cols: v *= np.repeat(np.exp2(rng.integers(-cols, cols + 1, shape[:-2] + (1, shape[-1] // 4))) * (rng.random(shape[:-2] + (1, shape[-1] // 4)) > 0.0625), 4, axis=-1).astype(np.float32)
    return mx_ref.flush(v.astype(BF))
C, STEP = 256, [1, 2, 4]
def numbers_of(rng):
    return {"x": np.array(f(rng, N, 128, 4 * C)), "u": np.array(f(rng, N, 128, 512)), "v": np.array(f(rng, N, 128, 512))}
def layers(rng):
    return np.array(f(rng, N, 128, 2048)).reshape(N, 8, 16, 4, 8, 16, 4)
def weights(rng, w):
    c, p = packed(np.ascontiguousarray(w).reshape(N, 128, 2048), rng)
    return {"wc": c, "ws": p}
def both(x, u):
    return {"x": x.astype(np.float32).reshape(N, 128, 4 * C).astype(BF), "u": u.astype(np.float32).reshape(N, 128, 512).astype(BF)}
def setup_inputs(rng):
    return {**numbers_of(rng), **weights(rng, layers(rng))}
def setup_inputs_ties(rng):
    d = numbers_of(rng)
    e = rng.permutation(N)
    x = rng.integers(-1, 2, (N, 128, C, 4)) * (rng.random((N, 128, C, 4)) < 0.09375)
    u = rng.integers(-1, 2, (N, 128, 128, 4)) * (rng.random((N, 128, 128, 4)) < 0.09375)
    x[e[0]] = x[e[0]][:, :1].copy()
    x[e[1]] = 0
    u[e[2]] = u[e[2]][:, :1].copy()
    w = np.zeros((N, 128, 512, 4), np.float32)
    for r in range(N):
        a, c = rng.permutation(512)[:128], rng.permutation(512)[:128]
        w[r, a // 4, c, a % 4] = 64
    return {**both(x, u), "v": d["v"], **weights(rng, w.astype(BF))}
def setup_inputs_near(rng):
    d = numbers_of(rng)
    h, o = rng.permutation(8), rng.permutation(N) % 4
    x = d["x"].astype(np.float32).reshape(N, 8, 16, C, 4)
    u = d["u"].astype(np.float32).reshape(N, 8, 16, 128, 4)
    x[:, :, 8:] = 0
    u[:, :, :8] = 0
    x[:, h[:2], :8] = 0
    p = np.exp2(np.arange(4) - 23.0)
    for r in range(N):
        k = 1.0 if o[r] < 2 else 2.0 ** -29
        if o[r] == 3:
            x[r, h[0], 0, :, 0] = rng.choice([1.0, 1.125], C) * 2.0 ** -30
            u[r, h[0], 0, :, 0] = rng.choice([1.125, 1.25], 128) * 2.0 ** -30
        else:
            x[r, h[0], 0, :, 0] = -1.0 if o[r] == 1 else 1.0
            u[r, h[0], 0, :, 0] = k
            x[r, h[1], 0] = ((rng.integers(0, 16, (C, 1)) >> np.arange(4)) & 1) * p
            u[r, h[1], 0] = k
            x[r, h[1], 1] = p
            u[r, h[1], 1] = ((rng.integers(0, 16, (128, 1)) >> np.arange(4)) & 1) * k
            x[r, h[1], 2, :, 0] = 2.0 ** -10
            u[r, h[1], 2, :, 0] = k
        x[r, h[0], 0, rng.integers(C), 0] = 2.0 ** 29
    w = layers(rng)
    w[:, h[:2], :8] = 0
    for g in h[:2]: w[:, :, :, :, g, :8] = 0
    return {**both(x, u), "v": d["v"], **weights(rng, w)}
def setup_inputs_huge(rng):
    d = numbers_of(rng)
    e = rng.permutation(N)
    x = 0.7 + 0.3 * rng.random((N, 8, 16, C, 4))
    u = 0.7 + 0.3 * rng.random((N, 8, 16, 128, 4))
    for i in range(N):
        r = e[i]
        if i == 0:
            x[r] = -0.94 - 0.06 * rng.random((8, 16, C, 4))
            x[r][:, :, rng.permutation(C)[:4]] *= -1.0
            u[r] = 0.94 + 0.06 * rng.random((8, 16, 128, 4))
        elif i % 2 == 1: u[r] *= -1.0
        else:
            x[r] *= rng.choice([-1.0, 1.0], (1, 1, C, 1))
            u[r] *= rng.choice([-1.0, 1.0], (1, 1, 128, 1))
    w = np.zeros((N, 128, 4, 128, 4), np.float32)
    i = np.arange(128)
    for b in range(4): w[:, i, b, i, b] = -1
    return {**both(x * 2.0 ** 30, u * 2.0 ** 30), "v": d["v"], **weights(rng, w.astype(BF))}
def setup_inputs_odd(rng):
    d = numbers_of(rng)
    x = d["x"].astype(np.float32).reshape(N, 8, 16, C, 4)
    u = d["u"].astype(np.float32).reshape(N, 8, 16, 128, 4)
    for a, n in ((x, C), (u, 128)):
        a[:, :, :8] = (2 * rng.integers(0, 8, (N, 8, 8, n, 4)) + 1) * rng.choice([-1.0, 1.0], (N, 8, 8, n, 4)) * 2.0 ** -16
        a[:, :, 0, :, 0] = rng.choice([1.625, 1.75, 1.875, 1.96875], (N, 8, n))
        a[:, :, 8] = 0
        a[:, :, 8, :, 0] = 1
    w = layers(rng)
    w[:, :, :, :, :, :9] = 0
    for g in range(8): w[:, g, 8, 0, g, 0, 0] = 3
    return {**both(x, u), "v": d["v"], **weights(rng, w)}
def setup_inputs_spread(rng):
    d = setup_inputs(rng)
    d["x"] = wide(rng, N, 128, 4 * C, cols=6)
    return d
def check_inputs(d):
    b = []
    for k in ("x", "u", "v"):
        a = np.abs(d[k].astype(np.float32))
        if not (np.isfinite(a).all() and ((a == 0) | (a >= 2.0 ** -30) & (a <= 2.0 ** 30)).all()): b.append("a value of " + k)
    none, least, most = [emit(mx_ref.quantize(np.full((128, 16), k, np.float32).astype(BF)))[1][0, 0] for k in (0.0, 2.0 ** -30, 2.0 ** 30)]
    for r in range(N):
        if ((d["wc"][r] == 0x7F) | (d["wc"][r] == 0xFF)).any(): b.append("wc: a code that is no number")
        s = mx_ref.live(d["ws"][r])
        if ((s != none) & ((s < least) | (s > most))).any(): b.append("ws: a scale out of range")
    return b
def reference(x, u, v, wc, ws):
    lay = [pk(wc[r], ws[r]) for r in range(N)]
    now = [mx_ref.quantize(x[r]) for r in range(N)]
    stat = [mx_ref.quantize(u[r]) for r in range(N)]
    down, along = np.zeros((N, 8, C), np.int64), np.zeros((N, 8, 128), np.int64)
    for h in STEP:
        sent = []
        for r in range(N):
            own = decode(now[r])
            s = mx_ref.matmul(stat[r], now[r]) + np.float32(0.0)
            down[r] = np.argmax(s.reshape(8, 16, C), axis=1) + 16 * np.arange(8)[:, None]
            along[r] = np.argsort(-s, axis=1, kind="stable")[:, :8].T
            a = gcols(decode(stat[r]).astype(BF), down[r]).astype(np.float32)
            z = mx_ref.quantize(((own + a) * np.float32(0.5)).astype(BF))
            now[r] = mx_ref.quantize(tile([mx_ref.matmul(pick(lay[r], np.arange(128 * b, 128 * b + 128)), z) * np.float32(0.03125) + own[:, b::4] for b in range(4)]))
            sent.append(mx_ref.quantize(gcols(decode(now[r]).astype(BF), along[r])))
        stat = [sent[(r - h) % N] for r in range(N)]
    y, op = np.zeros((N, 128, C), np.float32), np.zeros((N, 8, C + 128), np.float32)
    oc, osc = np.zeros((N, 128, 4 * C), np.uint8), np.zeros((N, 16, C), np.uint8)
    uc, usc = np.zeros((N, 128, 512), np.uint8), np.zeros((N, 16, 128), np.uint8)
    for r in range(N):
        y[r] = mx_ref.matmul(mx_ref.quantize(v[r]), now[r])
        op[r, :, :C] = down[r]
        op[r, :, C:] = along[r]
        oc[r], osc[r] = emit(now[r])
        uc[r], usc[r] = emit(stat[r])
    return {"y": y, "op": op, "oc": oc, "osc": osc, "uc": uc, "usc": usc}

@@ -1,0 +1,353 @@
+import numpy as np
+from concourse.mybir import dt, AluOpType, ActivationFunctionType
+
+ALU = AluOpType
+ACTF = ActivationFunctionType
+STEP = [1, 2, 4]
+BIG = 1.0e29
+
+SCRATCH = {
+    "xin": ("sbuf", [128, 1024], "bfloat16"),
+    "uin": ("sbuf", [128, 512], "bfloat16"),
+    "vin": ("sbuf", [128, 512], "bfloat16"),
+    "wq": ("sbuf", [128, 512], "float8_e4m3fn_x4"), "wp": ("sbuf", [128, 512], "uint8"),
+    "eh": ("sbuf", [128, 2048], "bfloat16"), "et": ("sbuf", [128, 2048], "bfloat16"),
+    "ehq": ("sbuf", [128, 512], "float8_e4m3fn_x4"), "ehp": ("sbuf", [128, 512], "uint8"),
+    "etq": ("sbuf", [128, 512], "float8_e4m3fn_x4"), "etp": ("sbuf", [128, 512], "uint8"),
+    "half": ("sbuf", [128, 512], "bfloat16"), "ioe": ("sbuf", [128, 512], "float32"),
+    "iob": ("sbuf", [128, 256], "bfloat16"),
+    "seg": ("sbuf", [128, 256], "float32"), "top": ("sbuf", [128, 256], "float32"),
+    "ib": ("sbuf", [128, 32], "int32"), "iw": ("sbuf", [128, 16], "int32"),
+    "base": ("sbuf", [128, 1], "float32"),
+    "dupl": ("sbuf", [128, 4], "uint16"), "seld": ("sbuf", [128, 2], "uint16"), "seln": ("sbuf", [128, 2], "uint16"),
+    "vcq": ("sbuf", [128, 128], "float8_e4m3fn_x4"), "vcp": ("sbuf", [128, 128], "uint8"),
+    "lu0": ("sbuf", [128, 128], "float8_e4m3fn_x4"), "ls0": ("sbuf", [128, 128], "uint8"),
+    "st": ("sbuf", [128, 256], "float32"), "rd": ("sbuf", [128, 264], "float32"),
+    "qd": ("sbuf", [128, 256], "bfloat16"), "cd": ("sbuf", [128, 256], "bfloat16"),
+    "kc": ("sbuf", [128, 32], "bfloat16"), "kt": ("sbuf", [128, 32], "bfloat16"),
+    "kd": ("sbuf", [128, 64], "bfloat16"), "ko": ("sbuf", [128, 64], "bfloat16"),
+    "offd": ("sbuf", [128, 16], "uint16"), "offn": ("sbuf", [128, 16], "uint16"),
+    "sc": ("sbuf", [128, 256], "float32"), "ra": ("sbuf", [128, 256], "float32"),
+    "junk": ("sbuf", [128, 256], "bfloat16"), "pen": ("sbuf", [128, 256], "bfloat16"),
+    "nb": ("sbuf", [128, 32], "float32"), "nt": ("sbuf", [128, 32], "float32"),
+    "nd": ("sbuf", [128, 64], "bfloat16"), "ngo": ("sbuf", [128, 64], "bfloat16"),
+    "du": ("sbuf", [128, 512], "bfloat16"), "tp": ("sbuf", [128, 1024], "bfloat16"),
+    "zt": ("sbuf", [128, 1024], "bfloat16"), "xt": ("sbuf", [128, 1024], "bfloat16"),
+    "vt": ("sbuf", [128, 512], "bfloat16"),
+    "opk": ("sbuf", [128, 256], "float32"), "opn": ("sbuf", [128, 128], "float32"),
+    "ysb": ("sbuf", [128, 256], "float32"),
+    "pd": ("psum", [128, 2048], "float32"), "pr": ("psum", [128, 2048], "float32"),
+}
+for _r in range(4):
+    SCRATCH["q%d" % _r] = ("sbuf", [128, 256], "float8_e4m3fn_x4")
+    SCRATCH["p%d" % _r] = ("sbuf", [128, 256], "uint8")
+for _r in range(3):
+    SCRATCH["zq%d" % _r] = ("sbuf", [128, 256], "float8_e4m3fn_x4")
+    SCRATCH["zp%d" % _r] = ("sbuf", [128, 256], "uint8")
+    SCRATCH["vq%d" % _r] = ("sbuf", [128, 128], "float8_e4m3fn_x4")
+    SCRATCH["vp%d" % _r] = ("sbuf", [128, 128], "uint8")
+    SCRATCH["lu%d" % (_r + 1)] = ("sbuf", [128, 128], "float8_e4m3fn_x4")
+    SCRATCH["ls%d" % (_r + 1)] = ("sbuf", [128, 128], "uint8")
+
+SEMAPHORES = ["sv", "sa", "sp", "sg"] + ["arr%d" % r for r in range(3)] + ["sent%d" % r for r in range(3)] + ["d%d" % k for k in range(24)]
+
+CYC = 0.00083 * 1.25
+WAKE = 0.07
+
+
+def rank_program(g, core, T, topo):
+    rank = T.rank_of(core)
+    if rank is None:
+        return
+    ops = []
+    last_w, readers = {}, {}
+    queue = {"V": g.vector, "A": g.scalar, "P": g.tensor, "G": g, "S": g.sync, "AD": g.scalar}
+    unit = {"V": "V", "A": "A", "P": "P", "G": "G", "S": "S", "AD": "A"}
+    csem = {"V": "sv", "A": "sa", "P": "sp", "G": "sg"}
+    ndma = [0]
+
+    def op(eng, cost, fn, reads=(), writes=(), sem=None, inc=1, extra=0.0):
+        k = len(ops)
+        hard, order = set(), set()
+        for b in reads:
+            if b in last_w:
+                hard.add(last_w[b])
+        for b in writes:
+            both = [last_w[b]] if b in last_w else []
+            both += readers.get(b, [])
+            for d in both:
+                if eng == "P" and ops[d]["eng"] == "P" and b[:2] in ("PD", "PR"):
+                    order.add(d)
+                else:
+                    hard.add(d)
+        for b in reads:
+            readers.setdefault(b, []).append(k)
+        for b in writes:
+            last_w[b] = k
+            readers[b] = []
+        ops.append({"k": k, "eng": eng, "u": unit[eng] if eng in unit else eng, "cost": cost, "extra": extra, "fn": fn,
+                    "hard": hard - {k}, "order": order - {k}, "sem": sem, "inc": inc})
+        return k
+
+    def V(n, fn, reads, writes, cyc=1.0):
+        return op("V", max(64, n * cyc) * CYC + 0.0, fn, reads, writes)
+
+    def GA(n, fn, reads, writes):
+        return op("V", 0.05 + n * 1.5 * CYC, fn, reads, writes)
+
+    def A(n, fn, reads, writes, fix=0.06):
+        return op("A", fix + n * CYC, fn, reads, writes)
+
+    def mm(out, lhs, rhs, n, start, stop, reads, bank):
+        return op("P", (n + 16) * CYC, lambda: g.tensor.matmul_mx(out, lhs[0], lhs[1], rhs[0], rhs[1], start, stop), reads, [bank])
+
+    def dma(eng, out, in_, reads, writes, lat=2.2):
+        s = "d%d" % ndma[0]
+        ndma[0] += 1
+        q = queue[eng]
+        return op(eng, 0.08, lambda: q.dma_start(out, in_), reads, writes, sem=s, inc=16, extra=lat)
+
+    def quant(q, p, t, n, reads, writes):
+        return op("V", 0.012 + 0.00022 * 4 * n * 1.25, lambda: g.vector.quantize_mx(q, p, t), reads, writes)
+
+    def cp(name, a, b):
+        return (T[name][:, a:b], T[{"q": "p", "z": "zp", "v": "vp"}[name[0]] + name[1:]][:, a:b])
+
+    tt, ts, tc = g.vector.tensor_tensor, g.vector.tensor_scalar, g.vector.tensor_copy
+    scan, act = g.vector.tensor_tensor_scan, g.scalar.activation
+    B4 = range(4)
+
+    dma("S", T.xin[:], T.x[:], [], ["xin"])
+    dma("AD", T.uin[:], T.u[:], [], ["uin"])
+    dma("S", T.wq[:].bitcast(dt.uint8), T.wc[:], [], ["wq"])
+    dma("AD", T.wp[:], T.ws[:], [], ["wp"])
+    dma("S", T.vin[:], T.v[:], [], ["vin"])
+
+    op("G", 0.2, lambda: g.iota(T.iw[:, 0:4], [[0, 4]], 0, 1), [], ["iw0"])
+    op("G", 0.2, lambda: g.iota(T.iw[:, 4:8], [[16, 2], [0, 2]], 0, 0), [], ["iw1"])
+    op("G", 1.2, lambda: g.iota(T.ioe[:], [[1, 512]], 0, -4, allow_small_or_imprecise_dtypes=True), [], ["ioe"])
+    V(256, lambda: g.vector.memset(T.half[:], 0.5), [], ["half"])
+    for b in (2, 3):
+        op("G", 1.3, lambda b=b: g.affine_select(T.eh[:, 512 * b:512 * b + 512], T.half[:], [[-1, 512]], ALU.is_equal, 0.0, b, 4),
+           ["half"], ["eh%d" % b])
+    op("G", 0.7, lambda: g.iota(T.iob[:], [[1, 256]], 0, 0, allow_small_or_imprecise_dtypes=True), [], ["iob"])
+    for b in (0, 1):
+        V(512, lambda b=b: ts(T.eh[:, 512 * b:512 * b + 512], T.ioe[:], float(b), 0.5, ALU.is_equal, ALU.mult), ["ioe"], ["eh%d" % b])
+    P1 = T.iw[:, 0:1]
+
+    def col(k):
+        return T.ib[:, k:k + 1]
+
+    def bit(k, src, srck, s1, o1, s2=None, o2=None):
+        if o2 is None:
+            V(1, lambda: ts(col(k), src, s1, None, o1), [srck], ["ib%d" % k])
+        else:
+            V(1, lambda: ts(col(k), src, s1, s2, o1, o2), [srck], ["ib%d" % k])
+
+    def add(k, a, b, o=ALU.add):
+        V(1, lambda: tt(col(k), col(a), col(b), o), ["ib%d" % a, "ib%d" % b], ["ib%d" % k])
+    V(1, lambda: ts(T.iw[:, 8:12], T.iw[:, 0:4], 15, None, ALU.bitwise_and), ["iw0"], ["iw2"])
+    V(1, lambda: tt(T.iw[:, 12:16], T.iw[:, 8:12], T.iw[:, 4:8], ALU.add), ["iw2", "iw1"], ["iw3"])
+    V(1, lambda: tc(T.dupl[:], T.iw[:, 12:16]), ["iw3"], ["dupl"])
+    bit(1, P1, "iw0", 1, ALU.bitwise_and)
+    bit(2, P1, "iw0", 14, ALU.bitwise_and)
+    bit(3, P1, "iw0", 4, ALU.logical_shift_right, 1, ALU.bitwise_and)
+    bit(4, P1, "iw0", 112, ALU.bitwise_and)
+    bit(5, P1, "iw0", 7, ALU.bitwise_and, 1, ALU.logical_shift_right)
+    bit(6, P1, "iw0", 5, ALU.logical_shift_right)
+    bit(7, P1, "iw0", 4, ALU.logical_shift_right)
+    bit(8, col(1), "ib1", 32, ALU.mult)
+    add(9, 2, 3)
+    add(10, 9, 8)
+    V(1, lambda: tc(T.seld[:, 0:1], col(10)), ["ib10"], ["seld"])
+    V(1, lambda: ts(T.base[:], col(4), 15.0, None, ALU.add), ["ib4"], ["base"])
+    add(11, 5, 6, ALU.subtract)
+    bit(13, col(11), "ib11", 3, ALU.bitwise_and)
+    bit(14, col(13), "ib13", 8, ALU.mult)
+    add(15, 14, 7)
+    add(16, 15, 8)
+    V(1, lambda: tc(T.seln[:, 0:1], col(16)), ["ib16"], ["seln"])
+    V(256, lambda: g.vector.memset(T.seg[:], BIG), [], ["seg0"])
+    V(16, lambda: g.vector.memset(T.seg[:, 0:256:16], -BIG), ["seg0"], ["seg0"])
+    V(256, lambda: g.vector.memset(T.top[:], BIG), [], ["top"])
+    V(1, lambda: g.vector.memset(T.rd[:, 0:1], 0.0), [], ["rd0"])
+    V(16, lambda: g.vector.memset(T.kc[:], 0.0), [], ["kc"])
+    EH = ["eh%d" % b for b in B4]
+    quant(T.ehq[:], T.ehp[:], T.eh[:], 512, EH, ["ehq"])
+    for k in (0, 1):
+        A(1024, lambda k=k: act(T.et[:, 1024 * k:1024 * k + 1024], T.eh[:, 1024 * k:1024 * k + 1024], ACTF.Copy, scale=64.0),
+          EH[2 * k:2 * k + 2], ["et%d" % k])
+    quant(T.etq[:], T.etp[:], T.et[:], 512, ["et0", "et1"], ["etq"])
+
+    quant(T.q0[:], T.p0[:], T.xin[:], 256, ["xin"], ["q0"])
+    quant(T.lu0[:], T.ls0[:], T.uin[:], 128, ["uin"], ["lu0"])
+
+    def unpack(r):
+        for b in B4:
+            mm(T.pd[:, 512 * b:512 * b + 256], (T.ehq[:, 128 * b:128 * b + 128], T.ehp[:, 128 * b:128 * b + 128]),
+               (T["q%d" % r][:], T["p%d" % r][:]), 256, True, True, ["ehq", "q%d" % r], "PD%d" % b)
+        for b in B4:
+            o, i = T.tp[:, 256 * b:256 * b + 256], T.pd[:, 512 * b:512 * b + 256]
+            if b in (0, 1, 2):
+                A(256, lambda o=o, i=i: act(o, i, ACTF.Copy), [], ["tp%d" % b, "PD%d" % b])
+            else:
+                V(256, lambda o=o, i=i: tc(o, i), [], ["tp%d" % b, "PD%d" % b])
+
+    unpack(0)
+    for r, h in enumerate(STEP):
+        Q = (T["q%d" % r][:], T["p%d" % r][:])
+        U = (T["lu%d" % r][:], T["ls%d" % r][:])
+        qn, un = "q%d" % r, "lu%d" % r
+        mm(T.pd[:, 0:256], U, Q, 256, True, True, [qn, un], "PD0")
+        for b in B4:
+            mm(T.pr[:, 512 * b:512 * b + 128], (T.ehq[:, 128 * b:128 * b + 128], T.ehp[:, 128 * b:128 * b + 128]), U, 128, True, True,
+               ["ehq", un], "PR%d" % b)
+        for b in B4:
+            A(128, lambda b=b: act(T.du[:, 128 * b:128 * b + 128], T.pr[:, 512 * b:512 * b + 128], ACTF.Copy), [], ["du%d" % b, "PR%d" % b])
+        for b in B4:
+            mm(T.pr[:, 512 * b:512 * b + 256], (T.etq[:, 128 * b:128 * b + 128], T.etp[:, 128 * b:128 * b + 128]), Q, 256, True, False,
+               ["etq", qn], "PR%d" % b)
+        V(256, lambda: g.vector.transpose(T.st[:], T.pd[:, 0:256]), [], ["st", "PD0"])
+        V(256, lambda: scan(T.rd[:, 1:257], T.seg[:], T.st[:], 0.0, ALU.min, ALU.max), ["seg0", "st"], ["rd"])
+        V(256, lambda: tt(T.qd[:], T.rd[:, 0:256], T.st[:], ALU.is_ge), ["rd", "rd0", "st"], ["qd"], 2.0)
+        V(256, lambda: scan(T.cd[:], T.qd[:], T.qd[:], 0.0, ALU.mult, ALU.add), ["qd"], ["cd"], 0.5)
+        V(16, lambda: ts(T.kc[:, 0:16], T.cd[:, 15:256:16], 15.0, None, ALU.min), ["cd"], ["kc"])
+        V(32, lambda: g.vector.transpose(T.kt[:], T.kc[:]), ["kc"], ["kt"])
+        GA(64, lambda: tc(T.kd[:], T.kt[:, 0:32].indirect(T.dupl[:, 0:4])), ["kt", "dupl"], ["kd"])
+        V(64, lambda: g.vector.transpose(T.ko[:], T.kd[:]), ["kd"], ["ko"])
+        GA(16, lambda: ts(T.offd[:], T.ko[:, 0:64].indirect(T.seld[:, 0:1]), -1.0, T.base[:], ALU.mult, ALU.add), ["ko", "seld", "base"], ["offd"])
+        for k in range(8):
+            if k == 0:
+                V(256, lambda: scan(T.ra[:], T.top[:], T.pd[:, 0:256], -2.0 * BIG, ALU.min, ALU.max), ["top"], ["ra", "PD0"])
+            else:
+                V(256, lambda: scan(T.ra[:], T.sc[:], T.sc[:], -2.0 * BIG, ALU.max, ALU.max), ["sc"], ["ra"])
+            A(256, lambda k=k: act(T.junk[:], T.ra[:], ACTF.Sign, bias=T.ra[:, 255:256], scale=-1.0, accum_out=T.nb[:, k:k + 1]),
+              ["ra"], ["junk", "nb%d" % k], 0.1)
+            if k < 7:
+                V(256, lambda k=k: ts(T.pen[:], T.iob[:], T.nb[:, k:k + 1], -BIG, ALU.is_equal, ALU.mult), ["iob", "nb%d" % k], ["pen"], 0.5)
+                if k == 0:
+                    V(256, lambda: tt(T.sc[:], T.pd[:, 0:256], T.pen[:], ALU.add), ["pen"], ["sc", "PD0"])
+                else:
+                    V(256, lambda: tt(T.sc[:], T.sc[:], T.pen[:], ALU.add), ["pen", "sc"], ["sc"], 2.0)
+        NB = ["nb%d" % k for k in range(8)]
+        for q in B4:
+            i, o = (q + 1) % 4, q
+            if q % 2:
+                A(8, lambda i=i, o=o: act(T.nb[32 * o:32 * o + 32, 8:16], T.nb[32 * i:32 * i + 32, 0:8], ACTF.Copy), NB, ["nx%d" % o])
+            else:
+                V(8, lambda i=i, o=o: tc(T.nb[32 * o:32 * o + 32, 8:16], T.nb[32 * i:32 * i + 32, 0:8]), NB, ["nx%d" % o])
+        NX = NB + ["nx%d" % q for q in B4]
+        V(16, lambda: tc(T.nb[0:64, 16:32], T.nb[64:128, 0:16]), NX, ["ny0"])
+        A(16, lambda: act(T.nb[64:128, 16:32], T.nb[0:64, 0:16], ACTF.Copy), NX, ["ny1"])
+        V(32, lambda: g.vector.transpose(T.nt[:], T.nb[:]), NX + ["ny0", "ny1"], ["nt"])
+        GA(64, lambda: tc(T.nd[:], T.nt[:, 0:32].indirect(T.dupl[:, 0:4])), ["nt", "dupl"], ["nd"])
+        V(64, lambda: g.vector.transpose(T.ngo[:], T.nd[:]), ["nd"], ["ngo"])
+        GA(16, lambda: tc(T.offn[:], T.ngo[:, 0:64].indirect(T.seln[:, 0:1])), ["ngo", "seln"], ["offn"])
+        for b in B4:
+            GA(256, lambda b=b: tt(T.zt[:, b:1024:4], T.du[:, 128 * b:128 * b + 128].indirect(T.offd[:, 0:16]), T.tp[:, 256 * b:256 * b + 256], ALU.add),
+               ["du%d" % b, "offd", "tp%d" % b], ["zt%d" % b])
+        quant(T["zq%d" % r][:], T["zp%d" % r][:], T.zt[:], 256, ["zt%d" % b for b in B4], ["zq%d" % r])
+        for b in B4:
+            mm(T.pr[:, 512 * b:512 * b + 256], (T.wq[:, 128 * b:128 * b + 128], T.wp[:, 128 * b:128 * b + 128]), (T["zq%d" % r][:], T["zp%d" % r][:]),
+               256, False, True, ["wq", "wp", "zq%d" % r], "PR%d" % b)
+        for b in B4:
+            o, i = T.xt[:, b:1024:4], T.pr[:, 512 * b:512 * b + 256]
+            if b in (0, 1, 2):
+                A(256, lambda o=o, i=i: act(o, i, ACTF.Copy, scale=0.03125), [], ["xt%d" % b, "PR%d" % b])
+            else:
+                V(256, lambda o=o, i=i: ts(o, i, 0.03125, None, ALU.mult), [], ["xt%d" % b, "PR%d" % b])
+        quant(T["q%d" % (r + 1)][:], T["p%d" % (r + 1)][:], T.xt[:], 256, ["xt%d" % b for b in B4], ["q%d" % (r + 1)])
+        unpack(r + 1)
+        for b in B4:
+            o, i = T.vt[:, b:512:4], T.tp[:, 256 * b:256 * b + 256].indirect(T.offn[:, 0:8])
+            if b in (0, 1):
+                op("A", 0.065 + 128 * 1.5 * CYC, lambda o=o, i=i: act(o, i, ACTF.Copy, scale=2.0), ["tp%d" % b, "offn"], ["vt%d" % b])
+            else:
+                GA(128, lambda o=o, i=i: ts(o, i, 2.0, None, ALU.mult), ["tp%d" % b, "offn"], ["vt%d" % b])
+        quant(T["vq%d" % r][:], T["vp%d" % r][:], T.vt[:], 128, ["vt%d" % b for b in B4], ["vq%d" % r])
+        dst = T.cores[(rank + h) % len(T.cores)]
+        ad = topo.addr(dst)
+        m = topo.mask(core, dst)
+        ne = len(topo.engines(core, dst))
+
+        def send(r=r, ad=ad, m=m):
+            a, s = T.sem["arr%d" % r], T.sem["sent%d" % r]
+            g.remote_dma(T["lu%d" % (r + 1)][:, 0:128].bitcast(dt.uint8), T["vq%d" % r][:, 0:128].bitcast(dt.uint8), a, s, ad[1], ad[0], m)
+            g.remote_dma(T["ls%d" % (r + 1)][:, 0:128], T["vp%d" % r][:, 0:128], a, s, ad[1], ad[0], m)
+            return None
+        op("G", 1.0, send, ["vq%d" % r], ["sent%d" % r], sem="sent%d" % r, inc=2 * ne)
+        op("N", 2.0, None, ["sent%d" % r], ["lu%d" % (r + 1)], sem="arr%d" % r, inc=2 * ne)
+        if r == 0:
+            quant(T.vcq[:], T.vcp[:], T.vin[:], 128, ["vin"], ["vcq"])
+    mm(T.pr[:, 0:256], (T.vcq[:], T.vcp[:]), (T.q3[:], T.p3[:]), 256, True, True, ["vcq", "q3"], "PR0")
+    A(256, lambda: act(T.ysb[:], T.pr[:, 0:256], ACTF.Copy), [], ["ysb", "PR0"])
+    dma("S", T.oc[:], T.q3[:].bitcast(dt.uint8), ["q3"], [])
+    for k in B4:
+        dma("S", T.osc[4 * k:4 * k + 4, :], T.p3[32 * k:32 * k + 4, :], ["q3"], [])
+    dma("S", T.y[:], T.ysb[:], ["ysb"], [])
+    op("A", 0.065 + 256 * 1.5 * CYC, lambda: act(T.opk[:], T.iob[:].indirect(T.offd[:, 0:16]), ACTF.Copy), ["iob", "offd"], ["opk"])
+    op("A", 0.065 + 128 * 1.5 * CYC, lambda: act(T.opn[:], T.iob[:].indirect(T.offn[:, 0:8]), ACTF.Copy), ["iob", "offn"], ["opn"])
+    dma("S", T["op"][:, 0:256], T.opk[0:128:16, :], ["opk"], [])
+    dma("S", T["op"][:, 256:384], T.opn[0:128:16, :], ["opn"], [])
+    dma("S", T.uc[:], T.lu3[:].bitcast(dt.uint8), ["lu3"], [])
+    for k in B4:
+        dma("AD" if k % 2 else "S", T.usc[4 * k:4 * k + 4, :], T.ls3[32 * k:32 * k + 4, :], ["lu3"], [])
+    plan_and_emit(g, T, ops, queue, csem)
+
+
+def plan_and_emit(g, T, ops, queue, csem):
+    n = len(ops)
+    succ = [[] for _ in range(n)]
+    for o in ops:
+        for d in o["hard"] | o["order"]:
+            succ[d].append(o["k"])
+    tail = [0.0] * n
+    for k in range(n - 1, -1, -1):
+        tail[k] = ops[k]["cost"] + ops[k]["extra"] + max([tail[s] + WAKE for s in succ[k]] + [0.0])
+    free, end, todo, seq = {}, {}, set(range(n)), []
+    left = [len(o["hard"] | o["order"]) for o in ops]
+    ready = {k for k in range(n) if left[k] == 0}
+    while ready:
+        est = {}
+        for k in ready:
+            o = ops[k]
+            t = max([free.get(o["u"], 0.0)] + [end[d] + WAKE for d in o["hard"]])
+            est[k] = t
+        lo = min(est.values())
+        k = max((k for k in ready if est[k] <= lo + 0.1), key=lambda k: (tail[k], -k))
+        o = ops[k]
+        free[o["u"]] = est[k] + o["cost"]
+        end[k] = est[k] + o["cost"] + o["extra"]
+        seq.append(k)
+        ready.discard(k)
+        for s in succ[k]:
+            left[s] -= 1
+            if left[s] == 0:
+                ready.add(s)
+    count, clock, after, total = {}, {}, {}, {}
+    for k in seq:
+        o = ops[k]
+        u = o["u"]
+        known = clock.setdefault(u, {})
+        need = {}
+        for d in sorted(o["hard"], key=lambda d: -seq.index(d)):
+            s, v = after[d][0]
+            if known.get(s, 0) >= v:
+                continue
+            need[s] = max(need.get(s, 0), v)
+            for a, b in after[d][1].items():
+                known[a] = max(known.get(a, 0), b)
+            known[s] = max(known.get(s, 0), v)
+        for s, v in need.items():
+            if o["fn"] is not None:
+                queue[o["eng"]].wait_ge(T.sem[s], v)
+        s = o["sem"] or csem[o["eng"]]
+        count[s] = count.get(s, 0) + o["inc"]
+        if o["fn"] is not None:
+            c = o["fn"]()
+            if c is not None:
+                c.then_inc(T.sem[s], o["inc"])
+        after[k] = ((s, count[s]), dict(known) if o["fn"] is not None else {})
+    for s, v in count.items():
+        if clock["G"].get(s, 0) < v:
+            g.wait_ge(T.sem[s], v)

@@ -1,55 +1,55 @@
-import numpy as np
 from concourse.mybir import dt, AluOpType, ActivationFunctionType
 
 ALU = AluOpType
 ACTF = ActivationFunctionType
 STEP = [1, 2, 4]
 BIG = 1.0e29
+ON_SCALAR = (1, 2, 3, 4, 5)
+XS, TS, RS, VS = "AAAV", "AAAA", "AAAV", "AAVV"
 
 SCRATCH = {
-    "xin": ("sbuf", [128, 1024], "bfloat16"),
-    "uin": ("sbuf", [128, 512], "bfloat16"),
-    "vin": ("sbuf", [128, 512], "bfloat16"),
+    "xin": ("sbuf", [128, 1024], "bfloat16"), "uin": ("sbuf", [128, 512], "bfloat16"), "vin": ("sbuf", [128, 512], "bfloat16"),
     "wq": ("sbuf", [128, 512], "float8_e4m3fn_x4"), "wp": ("sbuf", [128, 512], "uint8"),
-    "eh": ("sbuf", [128, 2048], "bfloat16"), "et": ("sbuf", [128, 2048], "bfloat16"),
+    "eh": ("sbuf", [128, 2048], "bfloat16"),
     "ehq": ("sbuf", [128, 512], "float8_e4m3fn_x4"), "ehp": ("sbuf", [128, 512], "uint8"),
-    "etq": ("sbuf", [128, 512], "float8_e4m3fn_x4"), "etp": ("sbuf", [128, 512], "uint8"),
-    "half": ("sbuf", [128, 512], "bfloat16"), "ioe": ("sbuf", [128, 512], "float32"),
-    "iob": ("sbuf", [128, 256], "bfloat16"),
-    "seg": ("sbuf", [128, 256], "float32"), "top": ("sbuf", [128, 256], "float32"),
-    "ib": ("sbuf", [128, 32], "int32"), "iw": ("sbuf", [128, 16], "int32"),
-    "base": ("sbuf", [128, 1], "float32"),
+    "full": ("sbuf", [128, 512], "bfloat16"), "ioe": ("sbuf", [128, 512], "float32"), "iob": ("sbuf", [128, 256], "bfloat16"),
+    "seg": ("sbuf", [128, 256], "float32"), "top": ("sbuf", [128, 256], "float32"), "ones": ("sbuf", [128, 256], "bfloat16"),
+    "ib": ("sbuf", [128, 32], "int32"), "iw": ("sbuf", [128, 16], "int32"), "base": ("sbuf", [128, 1], "float32"),
     "dupl": ("sbuf", [128, 4], "uint16"), "seld": ("sbuf", [128, 2], "uint16"), "seln": ("sbuf", [128, 2], "uint16"),
     "vcq": ("sbuf", [128, 128], "float8_e4m3fn_x4"), "vcp": ("sbuf", [128, 128], "uint8"),
-    "lu0": ("sbuf", [128, 128], "float8_e4m3fn_x4"), "ls0": ("sbuf", [128, 128], "uint8"),
     "st": ("sbuf", [128, 256], "float32"), "rd": ("sbuf", [128, 264], "float32"),
     "qd": ("sbuf", [128, 256], "bfloat16"), "cd": ("sbuf", [128, 256], "bfloat16"),
     "kc": ("sbuf", [128, 32], "bfloat16"), "kt": ("sbuf", [128, 32], "bfloat16"),
     "kd": ("sbuf", [128, 64], "bfloat16"), "ko": ("sbuf", [128, 64], "bfloat16"),
     "offd": ("sbuf", [128, 16], "uint16"), "offn": ("sbuf", [128, 16], "uint16"),
-    "sc": ("sbuf", [128, 256], "float32"), "ra": ("sbuf", [128, 256], "float32"),
-    "junk": ("sbuf", [128, 256], "bfloat16"), "pen": ("sbuf", [128, 256], "bfloat16"),
+    "ss": ("sbuf", [128, 256], "float32"), "rb": ("sbuf", [128, 8 * 264], "float32"),
+    "db0": ("sbuf", [128, 256], "float32"), "db1": ("sbuf", [128, 256], "float32"),
+    "neb": ("sbuf", [128, 2048], "bfloat16"), "sgb": ("sbuf", [128, 2048], "bfloat16"), "cb": ("sbuf", [128, 2048], "bfloat16"),
+    "junk": ("sbuf", [128, 256], "bfloat16"),
+    "n0": ("sbuf", [128, 1], "float32"), "jn": ("sbuf", [128, 8], "float32"), "jm": ("sbuf", [128, 8], "float32"),
     "nb": ("sbuf", [128, 32], "float32"), "nt": ("sbuf", [128, 32], "float32"),
     "nd": ("sbuf", [128, 64], "bfloat16"), "ngo": ("sbuf", [128, 64], "bfloat16"),
-    "du": ("sbuf", [128, 512], "bfloat16"), "tp": ("sbuf", [128, 1024], "bfloat16"),
-    "zt": ("sbuf", [128, 1024], "bfloat16"), "xt": ("sbuf", [128, 1024], "bfloat16"),
-    "vt": ("sbuf", [128, 512], "bfloat16"),
-    "opk": ("sbuf", [128, 256], "float32"), "opn": ("sbuf", [128, 128], "float32"),
-    "ysb": ("sbuf", [128, 256], "float32"),
+    "du": ("sbuf", [128, 512], "bfloat16"), "tp": ("sbuf", [128, 1024], "bfloat16"), "tr": ("sbuf", [128, 1024], "bfloat16"),
+    "zt": ("sbuf", [128, 1024], "bfloat16"), "xt": ("sbuf", [128, 1024], "bfloat16"), "vt": ("sbuf", [128, 512], "bfloat16"),
+    "opk": ("sbuf", [128, 256], "float32"), "opn": ("sbuf", [128, 128], "float32"), "ysb": ("sbuf", [128, 256], "float32"),
     "pd": ("psum", [128, 2048], "float32"), "pr": ("psum", [128, 2048], "float32"),
 }
-for _r in range(4):
-    SCRATCH["q%d" % _r] = ("sbuf", [128, 256], "float8_e4m3fn_x4")
-    SCRATCH["p%d" % _r] = ("sbuf", [128, 256], "uint8")
-for _r in range(3):
-    SCRATCH["zq%d" % _r] = ("sbuf", [128, 256], "float8_e4m3fn_x4")
-    SCRATCH["zp%d" % _r] = ("sbuf", [128, 256], "uint8")
-    SCRATCH["vq%d" % _r] = ("sbuf", [128, 128], "float8_e4m3fn_x4")
-    SCRATCH["vp%d" % _r] = ("sbuf", [128, 128], "uint8")
-    SCRATCH["lu%d" % (_r + 1)] = ("sbuf", [128, 128], "float8_e4m3fn_x4")
-    SCRATCH["ls%d" % (_r + 1)] = ("sbuf", [128, 128], "uint8")
 
-SEMAPHORES = ["sv", "sa", "sp", "sg"] + ["arr%d" % r for r in range(3)] + ["sent%d" % r for r in range(3)] + ["d%d" % k for k in range(24)]
+
+def _pair(name, plane, n):
+    SCRATCH[name] = ("sbuf", [128, n], "float8_e4m3fn_x4")
+    SCRATCH[plane] = ("sbuf", [128, n], "uint8")
+
+
+for _r in range(4):
+    _pair("q%d" % _r, "p%d" % _r, 256)
+    _pair("u%d" % _r, "s%d" % _r, 128)
+for _r in range(3):
+    _pair("zq%d" % _r, "zp%d" % _r, 256)
+    _pair("xl%d" % _r, "xs%d" % _r, 256)
+    SCRATCH["lo%d" % _r] = ("sbuf", [128, 8], "uint16")
+
+SEMAPHORES = ["sv", "sa", "sp", "sg"] + ["%s%d" % (n, r) for n in ("arr", "sent", "lst", "lsent") for r in range(3)] + ["d%d" % k for k in range(24)]
 
 CYC = 0.00083 * 1.25
 WAKE = 0.07
@@ -62,7 +62,6 @@ def rank_program(g, core, T, topo):
     ops = []
     last_w, readers = {}, {}
     queue = {"V": g.vector, "A": g.scalar, "P": g.tensor, "G": g, "S": g.sync, "AD": g.scalar}
-    unit = {"V": "V", "A": "A", "P": "P", "G": "G", "S": "S", "AD": "A"}
     csem = {"V": "sv", "A": "sa", "P": "sp", "G": "sg"}
     ndma = [0]
 
@@ -73,9 +72,7 @@ def rank_program(g, core, T, topo):
             if b in last_w:
                 hard.add(last_w[b])
         for b in writes:
-            both = [last_w[b]] if b in last_w else []
-            both += readers.get(b, [])
-            for d in both:
+            for d in ([last_w[b]] if b in last_w else []) + readers.get(b, []):
                 if eng == "P" and ops[d]["eng"] == "P" and b[:2] in ("PD", "PR"):
                     order.add(d)
                 else:
@@ -85,37 +82,40 @@ def rank_program(g, core, T, topo):
         for b in writes:
             last_w[b] = k
             readers[b] = []
-        ops.append({"k": k, "eng": eng, "u": unit[eng] if eng in unit else eng, "cost": cost, "extra": extra, "fn": fn,
-                    "hard": hard - {k}, "order": order - {k}, "sem": sem, "inc": inc})
-        return k
+        ops.append({"k": k, "eng": eng, "u": "A" if eng == "AD" else eng, "cost": cost, "extra": extra, "fn": fn,
+                    "hard": hard - {k}, "order": order - {k}, "sem": sem, "inc": inc, "w": list(writes)})
 
     def V(n, fn, reads, writes, cyc=1.0):
-        return op("V", max(64, n * cyc) * CYC + 0.0, fn, reads, writes)
+        op("V", max(64, n * cyc) * CYC, fn, reads, writes)
 
     def GA(n, fn, reads, writes):
-        return op("V", 0.05 + n * 1.5 * CYC, fn, reads, writes)
+        op("V", 0.05 + n * 1.5 * CYC, fn, reads, writes)
 
     def A(n, fn, reads, writes, fix=0.06):
-        return op("A", fix + n * CYC, fn, reads, writes)
+        op("A", fix + n * CYC, fn, reads, writes)
 
     def mm(out, lhs, rhs, n, start, stop, reads, bank):
-        return op("P", (n + 16) * CYC, lambda: g.tensor.matmul_mx(out, lhs[0], lhs[1], rhs[0], rhs[1], start, stop), reads, [bank])
+        op("P", (n + 16) * CYC, lambda: g.tensor.matmul_mx(out, lhs[0], lhs[1], rhs[0], rhs[1], start, stop), reads, [bank])
 
     def dma(eng, out, in_, reads, writes, lat=2.2):
         s = "d%d" % ndma[0]
         ndma[0] += 1
-        q = queue[eng]
-        return op(eng, 0.08, lambda: q.dma_start(out, in_), reads, writes, sem=s, inc=16, extra=lat)
+        op(eng, 0.08, lambda: queue[eng].dma_start(out, in_), reads, writes, sem=s, inc=16, extra=lat)
 
     def quant(q, p, t, n, reads, writes):
-        return op("V", 0.012 + 0.00022 * 4 * n * 1.25, lambda: g.vector.quantize_mx(q, p, t), reads, writes)
-
-    def cp(name, a, b):
-        return (T[name][:, a:b], T[{"q": "p", "z": "zp", "v": "vp"}[name[0]] + name[1:]][:, a:b])
+        op("V", 0.012 + 0.00022 * 4 * n * 1.25, lambda: g.vector.quantize_mx(q, p, t), reads, writes)
 
     tt, ts, tc = g.vector.tensor_tensor, g.vector.tensor_scalar, g.vector.tensor_copy
     scan, act = g.vector.tensor_tensor_scan, g.scalar.activation
     B4 = range(4)
+
+    def copy(e, o, i, n, reads, writes, scale=1.0):
+        if e == "A":
+            A(n, lambda: act(o, i, ACTF.Copy, scale=scale), reads, writes)
+        elif scale == 1.0:
+            V(n, lambda: tc(o, i), reads, writes)
+        else:
+            V(n, lambda: ts(o, i, scale, None, ALU.mult), reads, writes)
 
     dma("S", T.xin[:], T.x[:], [], ["xin"])
     dma("AD", T.uin[:], T.u[:], [], ["uin"])
@@ -124,15 +124,15 @@ def rank_program(g, core, T, topo):
     dma("S", T.vin[:], T.v[:], [], ["vin"])
 
     op("G", 0.2, lambda: g.iota(T.iw[:, 0:4], [[0, 4]], 0, 1), [], ["iw0"])
-    op("G", 0.2, lambda: g.iota(T.iw[:, 4:8], [[16, 2], [0, 2]], 0, 0), [], ["iw1"])
     op("G", 1.2, lambda: g.iota(T.ioe[:], [[1, 512]], 0, -4, allow_small_or_imprecise_dtypes=True), [], ["ioe"])
-    V(256, lambda: g.vector.memset(T.half[:], 0.5), [], ["half"])
-    for b in (2, 3):
-        op("G", 1.3, lambda b=b: g.affine_select(T.eh[:, 512 * b:512 * b + 512], T.half[:], [[-1, 512]], ALU.is_equal, 0.0, b, 4),
-           ["half"], ["eh%d" % b])
+    V(256, lambda: g.vector.memset(T.full[:], 32.0), [], ["full"])
+    op("G", 1.3, lambda: g.affine_select(T.eh[:, 1536:2048], T.full[:], [[-1, 512]], ALU.is_equal, 0.0, 3, 4), ["full"], ["eh3"])
+    op("G", 0.2, lambda: g.iota(T.iw[:, 4:8], [[16, 2], [0, 2]], 0, 0), [], ["iw1"])
     op("G", 0.7, lambda: g.iota(T.iob[:], [[1, 256]], 0, 0, allow_small_or_imprecise_dtypes=True), [], ["iob"])
-    for b in (0, 1):
-        V(512, lambda b=b: ts(T.eh[:, 512 * b:512 * b + 512], T.ioe[:], float(b), 0.5, ALU.is_equal, ALU.mult), ["ioe"], ["eh%d" % b])
+    for b in (0, 1, 2):
+        V(512, lambda b=b: ts(T.eh[:, 512 * b:512 * b + 512], T.ioe[:], float(b), 32.0, ALU.is_equal, ALU.mult), ["ioe"], ["eh%d" % b])
+    quant(T.ehq[:], T.ehp[:], T.eh[:], 512, ["eh%d" % b for b in B4], ["ehq"])
+
     P1 = T.iw[:, 0:1]
 
     def col(k):
@@ -170,43 +170,47 @@ def rank_program(g, core, T, topo):
     V(256, lambda: g.vector.memset(T.seg[:], BIG), [], ["seg0"])
     V(16, lambda: g.vector.memset(T.seg[:, 0:256:16], -BIG), ["seg0"], ["seg0"])
     V(256, lambda: g.vector.memset(T.top[:], BIG), [], ["top"])
+    V(8, lambda: g.vector.memset(T.rb[:, 0:8 * 264:264], -BIG), [], ["rbi"])
+    V(128, lambda: g.vector.memset(T.ones[:], 1.0), [], ["ones"])
+    V(1, lambda: g.vector.memset(T.jm[:, 0:1], 1.0), [], ["jm0"])
     V(1, lambda: g.vector.memset(T.rd[:, 0:1], 0.0), [], ["rd0"])
     V(16, lambda: g.vector.memset(T.kc[:], 0.0), [], ["kc"])
-    EH = ["eh%d" % b for b in B4]
-    quant(T.ehq[:], T.ehp[:], T.eh[:], 512, EH, ["ehq"])
-    for k in (0, 1):
-        A(1024, lambda k=k: act(T.et[:, 1024 * k:1024 * k + 1024], T.eh[:, 1024 * k:1024 * k + 1024], ACTF.Copy, scale=64.0),
-          EH[2 * k:2 * k + 2], ["et%d" % k])
-    quant(T.etq[:], T.etp[:], T.et[:], 512, ["et0", "et1"], ["etq"])
+
+    def W(name, b):
+        return (T[name + "q"][:, 128 * b:128 * b + 128], T[name + "p"][:, 128 * b:128 * b + 128])
 
     quant(T.q0[:], T.p0[:], T.xin[:], 256, ["xin"], ["q0"])
-    quant(T.lu0[:], T.ls0[:], T.uin[:], 128, ["uin"], ["lu0"])
+    quant(T.u0[:], T.s0[:], T.uin[:], 128, ["uin"], ["u0"])
 
-    def unpack(r):
+    def unpack(q, p, to, bank, BANK, how, scale):
         for b in B4:
-            mm(T.pd[:, 512 * b:512 * b + 256], (T.ehq[:, 128 * b:128 * b + 128], T.ehp[:, 128 * b:128 * b + 128]),
-               (T["q%d" % r][:], T["p%d" % r][:]), 256, True, True, ["ehq", "q%d" % r], "PD%d" % b)
+            mm(T[bank][:, 512 * b:512 * b + 256], W("eh", b), (T[q][:], T[p][:]), 256, True, True, ["ehq", q], BANK + "%d" % b)
         for b in B4:
-            o, i = T.tp[:, 256 * b:256 * b + 256], T.pd[:, 512 * b:512 * b + 256]
-            if b in (0, 1, 2):
-                A(256, lambda o=o, i=i: act(o, i, ACTF.Copy), [], ["tp%d" % b, "PD%d" % b])
-            else:
-                V(256, lambda o=o, i=i: tc(o, i), [], ["tp%d" % b, "PD%d" % b])
+            copy(how[b], T[to][:, 256 * b:256 * b + 256], T[bank][:, 512 * b:512 * b + 256], 256, [], ["%s%d" % (to, b), BANK + "%d" % b], scale)
 
-    unpack(0)
+    unpack("q0", "p0", "tp", "pr", "PR", TS, 0.015625)
     for r, h in enumerate(STEP):
-        Q = (T["q%d" % r][:], T["p%d" % r][:])
-        U = (T["lu%d" % r][:], T["ls%d" % r][:])
-        qn, un = "q%d" % r, "lu%d" % r
+        qn, un, q2, p2, u2, s2 = "q%d" % r, "u%d" % r, "q%d" % (r + 1), "p%d" % (r + 1), "u%d" % (r + 1), "s%d" % (r + 1)
+        Q, U = (T[qn][:], T["p%d" % r][:]), (T[un][:], T["s%d" % r][:])
+        Z = (T["zq%d" % r][:], T["zp%d" % r][:])
+        dst = T.cores[(rank + h) % len(T.cores)]
+        rid, pid, _ = topo.addr(dst)
+        m, ne = topo.mask(core, dst), len(topo.engines(core, dst))
+
+        def send(cost, lat, moves, reads, writes, arr, sent, rid=rid, pid=pid, m=m, ne=ne):
+            def go():
+                for o, i in moves:
+                    g.remote_dma(o, i, T.sem[arr], T.sem[sent], pid, rid, m)
+            op("G", cost, go, reads, [sent], sem=sent, inc=len(moves) * ne)
+            op("N", lat, None, [sent], writes, sem=arr, inc=len(moves) * ne)
+
         mm(T.pd[:, 0:256], U, Q, 256, True, True, [qn, un], "PD0")
         for b in B4:
-            mm(T.pr[:, 512 * b:512 * b + 128], (T.ehq[:, 128 * b:128 * b + 128], T.ehp[:, 128 * b:128 * b + 128]), U, 128, True, True,
-               ["ehq", un], "PR%d" % b)
+            k, bk, nm = (1 + b % 3, "pd", "PD") if r == 0 else (b, "pr", "PR")
+            mm(T[bk][:, 512 * k:512 * k + 128], W("eh", b), U, 128, True, True, ["ehq", un], "%s%d" % (nm, k))
+            copy("A", T.du[:, 128 * b:128 * b + 128], T[bk][:, 512 * k:512 * k + 128], 128, [], ["du%d" % b, "%s%d" % (nm, k)], 0.015625)
         for b in B4:
-            A(128, lambda b=b: act(T.du[:, 128 * b:128 * b + 128], T.pr[:, 512 * b:512 * b + 128], ACTF.Copy), [], ["du%d" % b, "PR%d" % b])
-        for b in B4:
-            mm(T.pr[:, 512 * b:512 * b + 256], (T.etq[:, 128 * b:128 * b + 128], T.etp[:, 128 * b:128 * b + 128]), Q, 256, True, False,
-               ["etq", qn], "PR%d" % b)
+            mm(T.pr[:, 512 * b:512 * b + 256], W("eh", b), Q, 256, True, False, ["ehq", qn], "PR%d" % b)
         V(256, lambda: g.vector.transpose(T.st[:], T.pd[:, 0:256]), [], ["st", "PD0"])
         V(256, lambda: scan(T.rd[:, 1:257], T.seg[:], T.st[:], 0.0, ALU.min, ALU.max), ["seg0", "st"], ["rd"])
         V(256, lambda: tt(T.qd[:], T.rd[:, 0:256], T.st[:], ALU.is_ge), ["rd", "rd0", "st"], ["qd"], 2.0)
@@ -216,71 +220,70 @@ def rank_program(g, core, T, topo):
         GA(64, lambda: tc(T.kd[:], T.kt[:, 0:32].indirect(T.dupl[:, 0:4])), ["kt", "dupl"], ["kd"])
         V(64, lambda: g.vector.transpose(T.ko[:], T.kd[:]), ["kd"], ["ko"])
         GA(16, lambda: ts(T.offd[:], T.ko[:, 0:64].indirect(T.seld[:, 0:1]), -1.0, T.base[:], ALU.mult, ALU.add), ["ko", "seld", "base"], ["offd"])
+        copy("A", T.ss[:], T.pd[:, 0:256], 256, [], ["ss", "PD0"])
         for k in range(8):
+            o = 264 * k
+            run, v = T.rb[:, o + 1:o + 257], T.rb[:, o + 256:o + 257]
             if k == 0:
-                V(256, lambda: scan(T.ra[:], T.top[:], T.pd[:, 0:256], -2.0 * BIG, ALU.min, ALU.max), ["top"], ["ra", "PD0"])
+                V(256, lambda run=run: scan(run, T.top[:], T.pd[:, 0:256], -2.0 * BIG, ALU.min, ALU.max), ["top"], ["rb0", "PD0"])
+                A(256, lambda run=run, v=v: act(T.junk[:], run, ACTF.Sign, bias=v, scale=-1.0, accum_out=T.n0[:]), ["rb0"], ["junk", "n0"], 0.1)
+                A(1, lambda: act(T.nb[:, 0:1], T.n0[:], ACTF.Identity, bias=-256.0, scale=2.0), ["n0"], ["nb0"])
+                continue
+            dk, ok = "db%d" % (k % 2), "db%d" % ((k - 1) % 2)
+            out, old, shifted = T[dk][:], T[ok][:], T.rb[:, o - 264:o - 8]
+            if k == 1:
+                V(256, lambda out=out, x=shifted: scan(out, x, T.pd[:, 0:256], -2.0 * BIG, ALU.max, ALU.min), ["rb0", "rbi"], [dk, "PD0"])
             else:
-                V(256, lambda: scan(T.ra[:], T.sc[:], T.sc[:], -2.0 * BIG, ALU.max, ALU.max), ["sc"], ["ra"])
-            A(256, lambda k=k: act(T.junk[:], T.ra[:], ACTF.Sign, bias=T.ra[:, 255:256], scale=-1.0, accum_out=T.nb[:, k:k + 1]),
-              ["ra"], ["junk", "nb%d" % k], 0.1)
+                V(256, lambda out=out, x=shifted, old=old: scan(out, x, old, -2.0 * BIG, ALU.max, ALU.min), ["rb%d" % (k - 1), "rbi", ok], [dk])
+            V(256, lambda out=out, run=run: scan(run, out, out, -2.0 * BIG, ALU.max, ALU.max), [dk, "rbi"], ["rb%d" % k])
+            V(1, lambda k=k, v=v, w=T.rb[:, o - 8:o - 7]: ts(T.jn[:, k:k + 1], v, w, T.jm[:, k - 1:k], ALU.is_equal, ALU.mult),
+              ["rb%d" % k, "rb%d" % (k - 1), "jm%d" % (k - 1)], ["jn%d" % k])
             if k < 7:
-                V(256, lambda k=k: ts(T.pen[:], T.iob[:], T.nb[:, k:k + 1], -BIG, ALU.is_equal, ALU.mult), ["iob", "nb%d" % k], ["pen"], 0.5)
-                if k == 0:
-                    V(256, lambda: tt(T.sc[:], T.pd[:, 0:256], T.pen[:], ALU.add), ["pen"], ["sc", "PD0"])
-                else:
-                    V(256, lambda: tt(T.sc[:], T.sc[:], T.pen[:], ALU.add), ["pen", "sc"], ["sc"], 2.0)
+                A(1, lambda k=k: act(T.jm[:, k:k + 1], T.jn[:, k:k + 1], ACTF.Identity, bias=1.0), ["jn%d" % k], ["jm%d" % k])
+            e, c, f = [T[x][:, 256 * k:256 * k + 256] for x in ("neb", "cb", "sgb")]
+            if k in ON_SCALAR:
+                A(256, lambda f=f, v=v: act(f, T.ss[:], ACTF.Sign, bias=v, scale=-1.0), ["ss", "rb%d" % k], ["sgb%d" % k])
+                A(256, lambda f=f, e=e: act(e, f, ACTF.Abs), ["sgb%d" % k], ["neb%d" % k])
+            else:
+                V(256, lambda e=e, v=v: ts(e, T.ss[:], v, None, ALU.not_equal), ["ss", "rb%d" % k], ["neb%d" % k])
+            V(256, lambda e=e, c=c, k=k: scan(c, e, T.ones[:], T.jn[:, k:k + 1], ALU.add, ALU.subtract), ["neb%d" % k, "jn%d" % k, "ones"], ["cb%d" % k], 0.5)
+            A(256, lambda c=c, k=k: act(T.junk[:], c, ACTF.Sign, bias=0.5, accum_out=T.nb[:, k:k + 1]), ["cb%d" % k], ["junk", "nb%d" % k], 0.1)
         NB = ["nb%d" % k for k in range(8)]
         for q in B4:
-            i, o = (q + 1) % 4, q
-            if q % 2:
-                A(8, lambda i=i, o=o: act(T.nb[32 * o:32 * o + 32, 8:16], T.nb[32 * i:32 * i + 32, 0:8], ACTF.Copy), NB, ["nx%d" % o])
-            else:
-                V(8, lambda i=i, o=o: tc(T.nb[32 * o:32 * o + 32, 8:16], T.nb[32 * i:32 * i + 32, 0:8]), NB, ["nx%d" % o])
+            copy("VA"[q % 2], T.nb[32 * q:32 * q + 32, 8:16], T.nb[32 * ((q + 1) % 4):32 * ((q + 1) % 4) + 32, 0:8], 8, NB, ["nx%d" % q])
         NX = NB + ["nx%d" % q for q in B4]
-        V(16, lambda: tc(T.nb[0:64, 16:32], T.nb[64:128, 0:16]), NX, ["ny0"])
-        A(16, lambda: act(T.nb[64:128, 16:32], T.nb[0:64, 0:16], ACTF.Copy), NX, ["ny1"])
+        copy("V", T.nb[0:64, 16:32], T.nb[64:128, 0:16], 16, NX, ["ny0"])
+        copy("A", T.nb[64:128, 16:32], T.nb[0:64, 0:16], 16, NX, ["ny1"])
         V(32, lambda: g.vector.transpose(T.nt[:], T.nb[:]), NX + ["ny0", "ny1"], ["nt"])
         GA(64, lambda: tc(T.nd[:], T.nt[:, 0:32].indirect(T.dupl[:, 0:4])), ["nt", "dupl"], ["nd"])
         V(64, lambda: g.vector.transpose(T.ngo[:], T.nd[:]), ["nd"], ["ngo"])
-        GA(16, lambda: tc(T.offn[:], T.ngo[:, 0:64].indirect(T.seln[:, 0:1])), ["ngo", "seln"], ["offn"])
+        GA(16, lambda: ts(T.offn[:], T.ngo[:, 0:64].indirect(T.seln[:, 0:1]), 0.5, 128.0, ALU.mult, ALU.add), ["ngo", "seln"], ["offn"])
+        send(0.5, 1.5, [(T["lo%d" % r][:], T.offn[:, 0:8])], ["offn"], ["lo%d" % r], "lst%d" % r, "lsent%d" % r)
         for b in B4:
             GA(256, lambda b=b: tt(T.zt[:, b:1024:4], T.du[:, 128 * b:128 * b + 128].indirect(T.offd[:, 0:16]), T.tp[:, 256 * b:256 * b + 256], ALU.add),
                ["du%d" % b, "offd", "tp%d" % b], ["zt%d" % b])
-        quant(T["zq%d" % r][:], T["zp%d" % r][:], T.zt[:], 256, ["zt%d" % b for b in B4], ["zq%d" % r])
+        quant(Z[0], Z[1], T.zt[:], 256, ["zt%d" % b for b in B4], ["zq%d" % r])
         for b in B4:
-            mm(T.pr[:, 512 * b:512 * b + 256], (T.wq[:, 128 * b:128 * b + 128], T.wp[:, 128 * b:128 * b + 128]), (T["zq%d" % r][:], T["zp%d" % r][:]),
-               256, False, True, ["wq", "wp", "zq%d" % r], "PR%d" % b)
+            mm(T.pr[:, 512 * b:512 * b + 256], W("w", b), Z, 256, False, True, ["wq", "wp", "zq%d" % r], "PR%d" % b)
         for b in B4:
-            o, i = T.xt[:, b:1024:4], T.pr[:, 512 * b:512 * b + 256]
-            if b in (0, 1, 2):
-                A(256, lambda o=o, i=i: act(o, i, ACTF.Copy, scale=0.03125), [], ["xt%d" % b, "PR%d" % b])
+            copy(XS[b], T.xt[:, b:1024:4], T.pr[:, 512 * b:512 * b + 256], 256, [], ["xt%d" % b, "PR%d" % b], 0.03125)
+        quant(T[q2][:], T[p2][:], T.xt[:], 256, ["xt%d" % b for b in B4], [q2])
+        send(1.0, 3.0, [(T["xl%d" % r][:].bitcast(dt.uint8), T[q2][:].bitcast(dt.uint8)), (T["xs%d" % r][:], T[p2][:])],
+             [q2], ["xl%d" % r], "arr%d" % r, "sent%d" % r)
+        unpack("xl%d" % r, "xs%d" % r, "tr", "pr", "PR", RS, 0.03125)
+        if r < 2:
+            unpack(q2, p2, "tp", "pd", "PD", TS, 0.015625)
+        for b in B4:
+            o, i = T.vt[:, b:512:4], T.tr[:, 256 * b:256 * b + 256].indirect(T["lo%d" % r][:, 0:8])
+            if VS[b] == "A":
+                op("A", 0.065 + 128 * 1.5 * CYC, lambda o=o, i=i: act(o, i, ACTF.Copy), ["tr%d" % b, "lo%d" % r], ["vt%d" % b])
             else:
-                V(256, lambda o=o, i=i: ts(o, i, 0.03125, None, ALU.mult), [], ["xt%d" % b, "PR%d" % b])
-        quant(T["q%d" % (r + 1)][:], T["p%d" % (r + 1)][:], T.xt[:], 256, ["xt%d" % b for b in B4], ["q%d" % (r + 1)])
-        unpack(r + 1)
-        for b in B4:
-            o, i = T.vt[:, b:512:4], T.tp[:, 256 * b:256 * b + 256].indirect(T.offn[:, 0:8])
-            if b in (0, 1):
-                op("A", 0.065 + 128 * 1.5 * CYC, lambda o=o, i=i: act(o, i, ACTF.Copy, scale=2.0), ["tp%d" % b, "offn"], ["vt%d" % b])
-            else:
-                GA(128, lambda o=o, i=i: ts(o, i, 2.0, None, ALU.mult), ["tp%d" % b, "offn"], ["vt%d" % b])
-        quant(T["vq%d" % r][:], T["vp%d" % r][:], T.vt[:], 128, ["vt%d" % b for b in B4], ["vq%d" % r])
-        dst = T.cores[(rank + h) % len(T.cores)]
-        ad = topo.addr(dst)
-        m = topo.mask(core, dst)
-        ne = len(topo.engines(core, dst))
-
-        def send(r=r, ad=ad, m=m):
-            a, s = T.sem["arr%d" % r], T.sem["sent%d" % r]
-            g.remote_dma(T["lu%d" % (r + 1)][:, 0:128].bitcast(dt.uint8), T["vq%d" % r][:, 0:128].bitcast(dt.uint8), a, s, ad[1], ad[0], m)
-            g.remote_dma(T["ls%d" % (r + 1)][:, 0:128], T["vp%d" % r][:, 0:128], a, s, ad[1], ad[0], m)
-            return None
-        op("G", 1.0, send, ["vq%d" % r], ["sent%d" % r], sem="sent%d" % r, inc=2 * ne)
-        op("N", 2.0, None, ["sent%d" % r], ["lu%d" % (r + 1)], sem="arr%d" % r, inc=2 * ne)
+                GA(128, lambda o=o, i=i: tc(o, i), ["tr%d" % b, "lo%d" % r], ["vt%d" % b])
+        quant(T[u2][:], T[s2][:], T.vt[:], 128, ["vt%d" % b for b in B4], [u2])
         if r == 0:
             quant(T.vcq[:], T.vcp[:], T.vin[:], 128, ["vin"], ["vcq"])
-    mm(T.pr[:, 0:256], (T.vcq[:], T.vcp[:]), (T.q3[:], T.p3[:]), 256, True, True, ["vcq", "q3"], "PR0")
-    A(256, lambda: act(T.ysb[:], T.pr[:, 0:256], ACTF.Copy), [], ["ysb", "PR0"])
+    mm(T.pd[:, 0:256], (T.vcq[:], T.vcp[:]), (T.q3[:], T.p3[:]), 256, True, True, ["vcq", "q3"], "PD0")
+    copy("A", T.ysb[:], T.pd[:, 0:256], 256, [], ["ysb", "PD0"])
     dma("S", T.oc[:], T.q3[:].bitcast(dt.uint8), ["q3"], [])
     for k in B4:
         dma("S", T.osc[4 * k:4 * k + 4, :], T.p3[32 * k:32 * k + 4, :], ["q3"], [])
@@ -289,9 +292,9 @@ def rank_program(g, core, T, topo):
     op("A", 0.065 + 128 * 1.5 * CYC, lambda: act(T.opn[:], T.iob[:].indirect(T.offn[:, 0:8]), ACTF.Copy), ["iob", "offn"], ["opn"])
     dma("S", T["op"][:, 0:256], T.opk[0:128:16, :], ["opk"], [])
     dma("S", T["op"][:, 256:384], T.opn[0:128:16, :], ["opn"], [])
-    dma("S", T.uc[:], T.lu3[:].bitcast(dt.uint8), ["lu3"], [])
+    dma("S", T.uc[:], T.u3[:].bitcast(dt.uint8), ["u3"], [])
     for k in B4:
-        dma("AD" if k % 2 else "S", T.usc[4 * k:4 * k + 4, :], T.ls3[32 * k:32 * k + 4, :], ["lu3"], [])
+        dma("AD" if k % 2 else "S", T.usc[4 * k:4 * k + 4, :], T.s3[32 * k:32 * k + 4, :], ["u3"], [])
     plan_and_emit(g, T, ops, queue, csem)
 
 
@@ -304,15 +307,11 @@ def plan_and_emit(g, T, ops, queue, csem):
     tail = [0.0] * n
     for k in range(n - 1, -1, -1):
         tail[k] = ops[k]["cost"] + ops[k]["extra"] + max([tail[s] + WAKE for s in succ[k]] + [0.0])
-    free, end, todo, seq = {}, {}, set(range(n)), []
+    free, end, seq = {}, {}, []
     left = [len(o["hard"] | o["order"]) for o in ops]
     ready = {k for k in range(n) if left[k] == 0}
     while ready:
-        est = {}
-        for k in ready:
-            o = ops[k]
-            t = max([free.get(o["u"], 0.0)] + [end[d] + WAKE for d in o["hard"]])
-            est[k] = t
+        est = {k: max([free.get(ops[k]["u"], 0.0)] + [end[d] + WAKE for d in ops[k]["hard"]]) for k in ready}
         lo = min(est.values())
         k = max((k for k in ready if est[k] <= lo + 0.1), key=lambda k: (tail[k], -k))
         o = ops[k]
@@ -324,22 +323,21 @@ def plan_and_emit(g, T, ops, queue, csem):
             left[s] -= 1
             if left[s] == 0:
                 ready.add(s)
-    count, clock, after, total = {}, {}, {}, {}
-    for k in seq:
+    count, clock, after = {}, {}, {}
+    for i, k in enumerate(seq):
         o = ops[k]
-        u = o["u"]
-        known = clock.setdefault(u, {})
+        known = clock.setdefault(o["u"], {})
         need = {}
-        for d in sorted(o["hard"], key=lambda d: -seq.index(d)):
-            s, v = after[d][0]
+        for d in sorted(o["hard"], key=lambda d: -after[d][2]):
+            s, v, _, seen = after[d]
             if known.get(s, 0) >= v:
                 continue
             need[s] = max(need.get(s, 0), v)
-            for a, b in after[d][1].items():
+            for a, b in seen.items():
                 known[a] = max(known.get(a, 0), b)
             known[s] = max(known.get(s, 0), v)
-        for s, v in need.items():
-            if o["fn"] is not None:
+        if o["fn"] is not None:
+            for s, v in need.items():
                 queue[o["eng"]].wait_ge(T.sem[s], v)
         s = o["sem"] or csem[o["eng"]]
         count[s] = count.get(s, 0) + o["inc"]
@@ -347,7 +345,7 @@ def plan_and_emit(g, T, ops, queue, csem):
             c = o["fn"]()
             if c is not None:
                 c.then_inc(T.sem[s], o["inc"])
-        after[k] = ((s, count[s]), dict(known) if o["fn"] is not None else {})
+        after[k] = (s, count[s], i, dict(known) if o["fn"] is not None else {})
     for s, v in count.items():
         if clock["G"].get(s, 0) < v:
             g.wait_ge(T.sem[s], v)

@@ -4,29 +4,27 @@ ALU = AluOpType
 ACTF = ActivationFunctionType
 STEP = [1, 2, 4]
 BIG = 1.0e29
-ON_SCALAR = (1, 2, 3, 4, 5)
-XS, TS, RS, VS = "AAAV", "AAAA", "AAAV", "AAVV"
+ON_SCALAR = (1, 2, 3, 4)
+TS, XS, RS, VS = "AAAA", "AAVV", "AAVV", "AAVV"
 
 SCRATCH = {
     "xin": ("sbuf", [128, 1024], "bfloat16"), "uin": ("sbuf", [128, 512], "bfloat16"), "vin": ("sbuf", [128, 512], "bfloat16"),
-    "wq": ("sbuf", [128, 512], "float8_e4m3fn_x4"), "wp": ("sbuf", [128, 512], "uint8"),
-    "eh": ("sbuf", [128, 2048], "bfloat16"),
-    "ehq": ("sbuf", [128, 512], "float8_e4m3fn_x4"), "ehp": ("sbuf", [128, 512], "uint8"),
-    "full": ("sbuf", [128, 512], "bfloat16"), "ioe": ("sbuf", [128, 512], "float32"), "iob": ("sbuf", [128, 256], "bfloat16"),
+    "eh": ("sbuf", [128, 2048], "bfloat16"), "full": ("sbuf", [128, 512], "bfloat16"), "ioe": ("sbuf", [128, 512], "float32"),
+    "iob": ("sbuf", [128, 256], "bfloat16"), "dist": ("sbuf", [128, 512], "float32"),
     "seg": ("sbuf", [128, 256], "float32"), "top": ("sbuf", [128, 256], "float32"), "ones": ("sbuf", [128, 256], "bfloat16"),
-    "ib": ("sbuf", [128, 32], "int32"), "iw": ("sbuf", [128, 16], "int32"), "base": ("sbuf", [128, 1], "float32"),
+    "ib": ("sbuf", [128, 16], "int32"), "fb": ("sbuf", [128, 8], "float32"), "iw": ("sbuf", [128, 8], "int32"), "base": ("sbuf", [128, 1], "float32"),
     "dupl": ("sbuf", [128, 4], "uint16"), "seld": ("sbuf", [128, 2], "uint16"), "seln": ("sbuf", [128, 2], "uint16"),
-    "vcq": ("sbuf", [128, 128], "float8_e4m3fn_x4"), "vcp": ("sbuf", [128, 128], "uint8"),
     "st": ("sbuf", [128, 256], "float32"), "rd": ("sbuf", [128, 264], "float32"),
     "qd": ("sbuf", [128, 256], "bfloat16"), "cd": ("sbuf", [128, 256], "bfloat16"),
     "kc": ("sbuf", [128, 32], "bfloat16"), "kt": ("sbuf", [128, 32], "bfloat16"),
     "kd": ("sbuf", [128, 64], "bfloat16"), "ko": ("sbuf", [128, 64], "bfloat16"),
     "offd": ("sbuf", [128, 16], "uint16"), "offn": ("sbuf", [128, 16], "uint16"),
-    "ss": ("sbuf", [128, 256], "float32"), "rb": ("sbuf", [128, 8 * 264], "float32"),
+    "rb": ("sbuf", [128, 8 * 264], "float32"),
     "db0": ("sbuf", [128, 256], "float32"), "db1": ("sbuf", [128, 256], "float32"),
     "neb": ("sbuf", [128, 2048], "bfloat16"), "sgb": ("sbuf", [128, 2048], "bfloat16"), "cb": ("sbuf", [128, 2048], "bfloat16"),
-    "junk": ("sbuf", [128, 256], "bfloat16"),
-    "n0": ("sbuf", [128, 1], "float32"), "jn": ("sbuf", [128, 8], "float32"), "jm": ("sbuf", [128, 8], "float32"),
+    "junk": ("sbuf", [128, 256], "bfloat16"), "n0": ("sbuf", [128, 1], "float32"),
+    "jn": ("sbuf", [128, 8], "float32"), "jm": ("sbuf", [128, 8], "float32"), "more": ("sbuf", [128, 8], "float32"),
+    "less": ("sbuf", [128, 8], "float32"), "part": ("sbuf", [128, 8], "float32"), "held": ("sbuf", [128, 8], "float32"),
     "nb": ("sbuf", [128, 32], "float32"), "nt": ("sbuf", [128, 32], "float32"),
     "nd": ("sbuf", [128, 64], "bfloat16"), "ngo": ("sbuf", [128, 64], "bfloat16"),
     "du": ("sbuf", [128, 512], "bfloat16"), "tp": ("sbuf", [128, 1024], "bfloat16"), "tr": ("sbuf", [128, 1024], "bfloat16"),
@@ -41,6 +39,9 @@ def _pair(name, plane, n):
     SCRATCH[plane] = ("sbuf", [128, n], "uint8")
 
 
+_pair("wq", "wp", 512)
+_pair("ehq", "ehp", 512)
+_pair("vcq", "vcp", 128)
 for _r in range(4):
     _pair("q%d" % _r, "p%d" % _r, 256)
     _pair("u%d" % _r, "s%d" % _r, 128)
@@ -94,8 +95,15 @@ def rank_program(g, core, T, topo):
     def A(n, fn, reads, writes, fix=0.06):
         op("A", fix + n * CYC, fn, reads, writes)
 
-    def mm(out, lhs, rhs, n, start, stop, reads, bank):
-        op("P", (n + 16) * CYC, lambda: g.tensor.matmul_mx(out, lhs[0], lhs[1], rhs[0], rhs[1], start, stop), reads, [bank])
+    def AG(n, fn, reads, writes):
+        op("A", 0.065 + n * 1.5 * CYC, fn, reads, writes)
+
+    def bank(b, n=256):
+        return T[b[0]][:, 512 * b[1]:512 * b[1] + n], b[0].upper() + "%d" % b[1]
+
+    def mm(b, lhs, rhs, n, start, stop, reads):
+        out, name = bank(b, n)
+        op("P", (n + 16) * CYC, lambda: g.tensor.matmul_mx(out, lhs[0], lhs[1], rhs[0], rhs[1], start, stop), reads, [name])
 
     def dma(eng, out, in_, reads, writes, lat=2.2):
         s = "d%d" % ndma[0]
@@ -129,50 +137,44 @@ def rank_program(g, core, T, topo):
     op("G", 1.3, lambda: g.affine_select(T.eh[:, 1536:2048], T.full[:], [[-1, 512]], ALU.is_equal, 0.0, 3, 4), ["full"], ["eh3"])
     op("G", 0.2, lambda: g.iota(T.iw[:, 4:8], [[16, 2], [0, 2]], 0, 0), [], ["iw1"])
     op("G", 0.7, lambda: g.iota(T.iob[:], [[1, 256]], 0, 0, allow_small_or_imprecise_dtypes=True), [], ["iob"])
-    for b in (0, 1, 2):
+    A(512, lambda: act(T.dist[:], T.ioe[:], ACTF.Abs, bias=-2.0), ["ioe"], ["dist"])
+    A(512, lambda: act(T.eh[:, 1024:1536], T.dist[:], ACTF.Relu, bias=32.0, scale=-32.0), ["dist"], ["eh2"])
+    for b in (0, 1):
         V(512, lambda b=b: ts(T.eh[:, 512 * b:512 * b + 512], T.ioe[:], float(b), 32.0, ALU.is_equal, ALU.mult), ["ioe"], ["eh%d" % b])
     quant(T.ehq[:], T.ehp[:], T.eh[:], 512, ["eh%d" % b for b in B4], ["ehq"])
-
-    P1 = T.iw[:, 0:1]
 
     def col(k):
         return T.ib[:, k:k + 1]
 
-    def bit(k, src, srck, s1, o1, s2=None, o2=None):
-        if o2 is None:
-            V(1, lambda: ts(col(k), src, s1, None, o1), [srck], ["ib%d" % k])
-        else:
-            V(1, lambda: ts(col(k), src, s1, s2, o1, o2), [srck], ["ib%d" % k])
+    def fcol(k):
+        return T.fb[:, k:k + 1]
 
-    def add(k, a, b, o=ALU.add):
-        V(1, lambda: tt(col(k), col(a), col(b), o), ["ib%d" % a, "ib%d" % b], ["ib%d" % k])
-    V(1, lambda: ts(T.iw[:, 8:12], T.iw[:, 0:4], 15, None, ALU.bitwise_and), ["iw0"], ["iw2"])
-    V(1, lambda: tt(T.iw[:, 12:16], T.iw[:, 8:12], T.iw[:, 4:8], ALU.add), ["iw2", "iw1"], ["iw3"])
-    V(1, lambda: tc(T.dupl[:], T.iw[:, 12:16]), ["iw3"], ["dupl"])
-    bit(1, P1, "iw0", 1, ALU.bitwise_and)
-    bit(2, P1, "iw0", 14, ALU.bitwise_and)
-    bit(3, P1, "iw0", 4, ALU.logical_shift_right, 1, ALU.bitwise_and)
-    bit(4, P1, "iw0", 112, ALU.bitwise_and)
-    bit(5, P1, "iw0", 7, ALU.bitwise_and, 1, ALU.logical_shift_right)
-    bit(6, P1, "iw0", 5, ALU.logical_shift_right)
-    bit(7, P1, "iw0", 4, ALU.logical_shift_right)
-    bit(8, col(1), "ib1", 32, ALU.mult)
-    add(9, 2, 3)
-    add(10, 9, 8)
-    V(1, lambda: tc(T.seld[:, 0:1], col(10)), ["ib10"], ["seld"])
-    V(1, lambda: ts(T.base[:], col(4), 15.0, None, ALU.add), ["ib4"], ["base"])
-    add(11, 5, 6, ALU.subtract)
-    bit(13, col(11), "ib11", 3, ALU.bitwise_and)
-    bit(14, col(13), "ib13", 8, ALU.mult)
-    add(15, 14, 7)
-    add(16, 15, 8)
-    V(1, lambda: tc(T.seln[:, 0:1], col(16)), ["ib16"], ["seln"])
-    V(256, lambda: g.vector.memset(T.seg[:], BIG), [], ["seg0"])
-    V(16, lambda: g.vector.memset(T.seg[:, 0:256:16], -BIG), ["seg0"], ["seg0"])
-    V(256, lambda: g.vector.memset(T.top[:], BIG), [], ["top"])
+    def bit(k, s1, o1, s2=None, o2=None):
+        if o2 is None:
+            V(1, lambda: ts(col(k), T.iw[:, 0:1], s1, None, o1), ["iw0"], ["ib%d" % k])
+        else:
+            V(1, lambda: ts(col(k), T.iw[:, 0:1], s1, s2, o1, o2), ["iw0"], ["ib%d" % k])
+    bit(0, 15, ALU.bitwise_and)
+    bit(1, 1, ALU.bitwise_and)
+    bit(2, 4, ALU.logical_shift_right, 1, ALU.bitwise_and)
+    bit(3, 7, ALU.bitwise_and, 1, ALU.logical_shift_right)
+    bit(4, 5, ALU.logical_shift_right)
+    bit(5, 4, ALU.logical_shift_right)
+    V(1, lambda: tc(fcol(0), col(0)), ["ib0"], ["fb0"])
+    V(1, lambda: ts(T.dupl[:], T.iw[:, 4:8], fcol(0), None, ALU.add), ["fb0", "iw1"], ["dupl"])
+    V(1, lambda: tt(fcol(1), col(0), col(2), ALU.add), ["ib0", "ib2"], ["fb1"])
+    V(1, lambda: ts(T.seld[:, 0:1], col(1), 31.0, fcol(1), ALU.mult, ALU.add), ["ib1", "fb1"], ["seld"])
+    V(1, lambda: tc(fcol(2), col(5)), ["ib5"], ["fb2"])
+    V(1, lambda: ts(T.base[:], col(5), 16.0, 15.0, ALU.mult, ALU.add), ["ib5"], ["base"])
+    V(1, lambda: tt(col(7), col(3), col(4), ALU.subtract), ["ib3", "ib4"], ["ib7"])
+    V(1, lambda: ts(col(8), col(7), 3, None, ALU.bitwise_and), ["ib7"], ["ib8"])
+    V(1, lambda: ts(fcol(3), col(8), 8.0, fcol(2), ALU.mult, ALU.add), ["ib8", "fb2"], ["fb3"])
+    V(1, lambda: ts(T.seln[:, 0:1], col(1), 32.0, fcol(3), ALU.mult, ALU.add), ["ib1", "fb3"], ["seln"])
+    A(256, lambda: act(T.top[:], T.ioe[:, 0:256], ACTF.Identity, bias=BIG, scale=0.0), ["ioe"], ["top"])
+    A(256, lambda: act(T.seg[:], T.ioe[:, 0:256], ACTF.Identity, bias=BIG, scale=0.0), ["ioe"], ["seg0"])
+    A(16, lambda: act(T.seg[:, 0:256:16], T.ioe[:, 0:16], ACTF.Identity, bias=-BIG, scale=0.0), ["ioe", "seg0"], ["seg0"])
+    A(256, lambda: act(T.ones[:], T.ioe[:, 0:256], ACTF.Identity, bias=1.0, scale=0.0), ["ioe"], ["ones"])
     V(8, lambda: g.vector.memset(T.rb[:, 0:8 * 264:264], -BIG), [], ["rbi"])
-    V(128, lambda: g.vector.memset(T.ones[:], 1.0), [], ["ones"])
-    V(1, lambda: g.vector.memset(T.jm[:, 0:1], 1.0), [], ["jm0"])
     V(1, lambda: g.vector.memset(T.rd[:, 0:1], 0.0), [], ["rd0"])
     V(16, lambda: g.vector.memset(T.kc[:], 0.0), [], ["kc"])
 
@@ -182,13 +184,14 @@ def rank_program(g, core, T, topo):
     quant(T.q0[:], T.p0[:], T.xin[:], 256, ["xin"], ["q0"])
     quant(T.u0[:], T.s0[:], T.uin[:], 128, ["uin"], ["u0"])
 
-    def unpack(q, p, to, bank, BANK, how, scale):
+    def unpack(q, p, to, at, how, scale):
         for b in B4:
-            mm(T[bank][:, 512 * b:512 * b + 256], W("eh", b), (T[q][:], T[p][:]), 256, True, True, ["ehq", q], BANK + "%d" % b)
+            mm((at, b), W("eh", b), (T[q][:], T[p][:]), 256, True, True, ["ehq", q])
         for b in B4:
-            copy(how[b], T[to][:, 256 * b:256 * b + 256], T[bank][:, 512 * b:512 * b + 256], 256, [], ["%s%d" % (to, b), BANK + "%d" % b], scale)
+            i, bn = bank((at, b))
+            copy(how[b], T[to][:, 256 * b:256 * b + 256], i, 256, [], ["%s%d" % (to, b), bn], scale)
 
-    unpack("q0", "p0", "tp", "pr", "PR", TS, 0.015625)
+    unpack("q0", "p0", "tp", "pr", TS, 0.015625)
     for r, h in enumerate(STEP):
         qn, un, q2, p2, u2, s2 = "q%d" % r, "u%d" % r, "q%d" % (r + 1), "p%d" % (r + 1), "u%d" % (r + 1), "s%d" % (r + 1)
         Q, U = (T[qn][:], T["p%d" % r][:]), (T[un][:], T["s%d" % r][:])
@@ -204,13 +207,15 @@ def rank_program(g, core, T, topo):
             op("G", cost, go, reads, [sent], sem=sent, inc=len(moves) * ne)
             op("N", lat, None, [sent], writes, sem=arr, inc=len(moves) * ne)
 
-        mm(T.pd[:, 0:256], U, Q, 256, True, True, [qn, un], "PD0")
+        mm(("pd", 0), U, Q, 256, True, True, [qn, un])
+        mm(("pd", 1), U, Q, 256, True, True, [qn, un])
         for b in B4:
-            k, bk, nm = (1 + b % 3, "pd", "PD") if r == 0 else (b, "pr", "PR")
-            mm(T[bk][:, 512 * k:512 * k + 128], W("eh", b), U, 128, True, True, ["ehq", un], "%s%d" % (nm, k))
-            copy("A", T.du[:, 128 * b:128 * b + 128], T[bk][:, 512 * k:512 * k + 128], 128, [], ["du%d" % b, "%s%d" % (nm, k)], 0.015625)
+            at = ("pd", 2 + b % 2) if r == 0 else ("pr", b)
+            mm(at, W("eh", b), U, 128, True, True, ["ehq", un])
+            i, bn = bank(at, 128)
+            copy("A", T.du[:, 128 * b:128 * b + 128], i, 128, [], ["du%d" % b, bn], 0.015625)
         for b in B4:
-            mm(T.pr[:, 512 * b:512 * b + 256], W("eh", b), Q, 256, True, False, ["ehq", qn], "PR%d" % b)
+            mm(("pr", b), W("eh", b), Q, 256, True, False, ["ehq", qn])
         V(256, lambda: g.vector.transpose(T.st[:], T.pd[:, 0:256]), [], ["st", "PD0"])
         V(256, lambda: scan(T.rd[:, 1:257], T.seg[:], T.st[:], 0.0, ALU.min, ALU.max), ["seg0", "st"], ["rd"])
         V(256, lambda: tt(T.qd[:], T.rd[:, 0:256], T.st[:], ALU.is_ge), ["rd", "rd0", "st"], ["qd"], 2.0)
@@ -220,10 +225,21 @@ def rank_program(g, core, T, topo):
         GA(64, lambda: tc(T.kd[:], T.kt[:, 0:32].indirect(T.dupl[:, 0:4])), ["kt", "dupl"], ["kd"])
         V(64, lambda: g.vector.transpose(T.ko[:], T.kd[:]), ["kd"], ["ko"])
         GA(16, lambda: ts(T.offd[:], T.ko[:, 0:64].indirect(T.seld[:, 0:1]), -1.0, T.base[:], ALU.mult, ALU.add), ["ko", "seld", "base"], ["offd"])
-        copy("A", T.ss[:], T.pd[:, 0:256], 256, [], ["ss", "PD0"])
+        for b in B4:
+            GA(256, lambda b=b: tt(T.zt[:, b:1024:4], T.du[:, 128 * b:128 * b + 128].indirect(T.offd[:, 0:16]), T.tp[:, 256 * b:256 * b + 256], ALU.add),
+               ["du%d" % b, "offd", "tp%d" % b], ["zt%d" % b])
+        quant(Z[0], Z[1], T.zt[:], 256, ["zt%d" % b for b in B4], ["zq%d" % r])
+        for b in B4:
+            mm(("pr", b), W("w", b), Z, 256, False, True, ["wq", "wp", "zq%d" % r])
+        for b in B4:
+            i, bn = bank(("pr", b))
+            copy(XS[b], T.xt[:, b:1024:4], i, 256, [], ["xt%d" % b, bn], 0.03125)
+        quant(T[q2][:], T[p2][:], T.xt[:], 256, ["xt%d" % b for b in B4], [q2])
+        send(1.0, 3.0, [(T["xl%d" % r][:].bitcast(dt.uint8), T[q2][:].bitcast(dt.uint8)), (T["xs%d" % r][:], T[p2][:])],
+             [q2], ["xl%d" % r], "arr%d" % r, "sent%d" % r)
         for k in range(8):
-            o = 264 * k
-            run, v = T.rb[:, o + 1:o + 257], T.rb[:, o + 256:o + 257]
+            o, kk = 264 * k, slice(k, k + 1)
+            run, v, w = T.rb[:, o + 1:o + 257], T.rb[:, o + 256:o + 257], T.rb[:, o - 8:o - 7]
             if k == 0:
                 V(256, lambda run=run: scan(run, T.top[:], T.pd[:, 0:256], -2.0 * BIG, ALU.min, ALU.max), ["top"], ["rb0", "PD0"])
                 A(256, lambda run=run, v=v: act(T.junk[:], run, ACTF.Sign, bias=v, scale=-1.0, accum_out=T.n0[:]), ["rb0"], ["junk", "n0"], 0.1)
@@ -236,18 +252,27 @@ def rank_program(g, core, T, topo):
             else:
                 V(256, lambda out=out, x=shifted, old=old: scan(out, x, old, -2.0 * BIG, ALU.max, ALU.min), ["rb%d" % (k - 1), "rbi", ok], [dk])
             V(256, lambda out=out, run=run: scan(run, out, out, -2.0 * BIG, ALU.max, ALU.max), [dk, "rbi"], ["rb%d" % k])
-            V(1, lambda k=k, v=v, w=T.rb[:, o - 8:o - 7]: ts(T.jn[:, k:k + 1], v, w, T.jm[:, k - 1:k], ALU.is_equal, ALU.mult),
-              ["rb%d" % k, "rb%d" % (k - 1), "jm%d" % (k - 1)], ["jn%d" % k])
-            if k < 7:
-                A(1, lambda k=k: act(T.jm[:, k:k + 1], T.jn[:, k:k + 1], ACTF.Identity, bias=1.0), ["jn%d" % k], ["jm%d" % k])
             e, c, f = [T[x][:, 256 * k:256 * k + 256] for x in ("neb", "cb", "sgb")]
             if k in ON_SCALAR:
-                A(256, lambda f=f, v=v: act(f, T.ss[:], ACTF.Sign, bias=v, scale=-1.0), ["ss", "rb%d" % k], ["sgb%d" % k])
-                A(256, lambda f=f, e=e: act(e, f, ACTF.Abs), ["sgb%d" % k], ["neb%d" % k])
+                A(256, lambda f=f, v=v, kk=kk: act(f, T.pd[:, 512:768], ACTF.Sign, bias=v, scale=-1.0, accum_out=T.less[:, kk]),
+                  ["rb%d" % k], ["sgb%d" % k, "less%d" % k, "PD1"], 0.08)
+                A(256, lambda f=f, e=e, kk=kk: act(e, f, ACTF.Abs, accum_out=T.more[:, kk]), ["sgb%d" % k], ["neb%d" % k, "more%d" % k], 0.08)
+                A(1, lambda k=k, kk=kk: act(T.part[:, kk], T.less[:, kk], ACTF.Identity, bias=k + 0.5, scale=0.5), ["less%d" % k], ["part%d" % k])
+                A(1, lambda kk=kk: act(T.held[:, kk], T.more[:, kk], ACTF.Identity, bias=T.part[:, kk], scale=-0.5),
+                  ["more%d" % k, "part%d" % k], ["held%d" % k])
+                first, half, need = 0.0, T.held[:, kk], []
+                if k < 7 and k + 1 not in ON_SCALAR:
+                    A(1, lambda kk=kk: act(T.jm[:, kk], T.held[:, kk], ACTF.Identity, bias=0.5), ["held%d" % k], ["jm%d" % k])
             else:
-                V(256, lambda e=e, v=v: ts(e, T.ss[:], v, None, ALU.not_equal), ["ss", "rb%d" % k], ["neb%d" % k])
-            V(256, lambda e=e, c=c, k=k: scan(c, e, T.ones[:], T.jn[:, k:k + 1], ALU.add, ALU.subtract), ["neb%d" % k, "jn%d" % k, "ones"], ["cb%d" % k], 0.5)
-            A(256, lambda c=c, k=k: act(T.junk[:], c, ACTF.Sign, bias=0.5, accum_out=T.nb[:, k:k + 1]), ["cb%d" % k], ["junk", "nb%d" % k], 0.1)
+                V(256, lambda e=e, v=v: ts(e, T.pd[:, 0:256], v, None, ALU.not_equal), ["rb%d" % k], ["neb%d" % k, "PD0"])
+                V(1, lambda v=v, w=w, k=k, kk=kk: ts(T.jn[:, kk], v, w, T.jm[:, k - 1:k], ALU.is_equal, ALU.mult),
+                  ["rb%d" % k, "rb%d" % (k - 1), "jm%d" % (k - 1)], ["jn%d" % k])
+                if k < 7 and k + 1 not in ON_SCALAR:
+                    A(1, lambda kk=kk: act(T.jm[:, kk], T.jn[:, kk], ACTF.Identity, bias=1.0), ["jn%d" % k], ["jm%d" % k])
+                first, half, need = T.jn[:, kk], 0.5, ["jn%d" % k]
+            V(256, lambda e=e, c=c, first=first: scan(c, e, T.ones[:], first, ALU.add, ALU.subtract), ["neb%d" % k, "ones"] + need, ["cb%d" % k], 0.5)
+            A(256, lambda c=c, kk=kk, half=half: act(T.junk[:], c, ACTF.Sign, bias=half, accum_out=T.nb[:, kk]),
+              ["cb%d" % k] + ([] if need else ["held%d" % k]), ["junk", "nb%d" % k], 0.1)
         NB = ["nb%d" % k for k in range(8)]
         for q in B4:
             copy("VA"[q % 2], T.nb[32 * q:32 * q + 32, 8:16], T.nb[32 * ((q + 1) % 4):32 * ((q + 1) % 4) + 32, 0:8], 8, NB, ["nx%d" % q])
@@ -259,37 +284,26 @@ def rank_program(g, core, T, topo):
         V(64, lambda: g.vector.transpose(T.ngo[:], T.nd[:]), ["nd"], ["ngo"])
         GA(16, lambda: ts(T.offn[:], T.ngo[:, 0:64].indirect(T.seln[:, 0:1]), 0.5, 128.0, ALU.mult, ALU.add), ["ngo", "seln"], ["offn"])
         send(0.5, 1.5, [(T["lo%d" % r][:], T.offn[:, 0:8])], ["offn"], ["lo%d" % r], "lst%d" % r, "lsent%d" % r)
-        for b in B4:
-            GA(256, lambda b=b: tt(T.zt[:, b:1024:4], T.du[:, 128 * b:128 * b + 128].indirect(T.offd[:, 0:16]), T.tp[:, 256 * b:256 * b + 256], ALU.add),
-               ["du%d" % b, "offd", "tp%d" % b], ["zt%d" % b])
-        quant(Z[0], Z[1], T.zt[:], 256, ["zt%d" % b for b in B4], ["zq%d" % r])
-        for b in B4:
-            mm(T.pr[:, 512 * b:512 * b + 256], W("w", b), Z, 256, False, True, ["wq", "wp", "zq%d" % r], "PR%d" % b)
-        for b in B4:
-            copy(XS[b], T.xt[:, b:1024:4], T.pr[:, 512 * b:512 * b + 256], 256, [], ["xt%d" % b, "PR%d" % b], 0.03125)
-        quant(T[q2][:], T[p2][:], T.xt[:], 256, ["xt%d" % b for b in B4], [q2])
-        send(1.0, 3.0, [(T["xl%d" % r][:].bitcast(dt.uint8), T[q2][:].bitcast(dt.uint8)), (T["xs%d" % r][:], T[p2][:])],
-             [q2], ["xl%d" % r], "arr%d" % r, "sent%d" % r)
-        unpack("xl%d" % r, "xs%d" % r, "tr", "pr", "PR", RS, 0.03125)
+        unpack("xl%d" % r, "xs%d" % r, "tr", "pr", RS, 0.03125)
         if r < 2:
-            unpack(q2, p2, "tp", "pd", "PD", TS, 0.015625)
+            unpack(q2, p2, "tp", "pd", TS, 0.015625)
         for b in B4:
             o, i = T.vt[:, b:512:4], T.tr[:, 256 * b:256 * b + 256].indirect(T["lo%d" % r][:, 0:8])
             if VS[b] == "A":
-                op("A", 0.065 + 128 * 1.5 * CYC, lambda o=o, i=i: act(o, i, ACTF.Copy), ["tr%d" % b, "lo%d" % r], ["vt%d" % b])
+                AG(128, lambda o=o, i=i: act(o, i, ACTF.Copy), ["tr%d" % b, "lo%d" % r], ["vt%d" % b])
             else:
                 GA(128, lambda o=o, i=i: tc(o, i), ["tr%d" % b, "lo%d" % r], ["vt%d" % b])
         quant(T[u2][:], T[s2][:], T.vt[:], 128, ["vt%d" % b for b in B4], [u2])
         if r == 0:
             quant(T.vcq[:], T.vcp[:], T.vin[:], 128, ["vin"], ["vcq"])
-    mm(T.pd[:, 0:256], (T.vcq[:], T.vcp[:]), (T.q3[:], T.p3[:]), 256, True, True, ["vcq", "q3"], "PD0")
-    copy("A", T.ysb[:], T.pd[:, 0:256], 256, [], ["ysb", "PD0"])
+    mm(("pd", 2), (T.vcq[:], T.vcp[:]), (T.q3[:], T.p3[:]), 256, True, True, ["vcq", "q3"])
+    copy("A", T.ysb[:], bank(("pd", 2))[0], 256, [], ["ysb", "PD2"])
     dma("S", T.oc[:], T.q3[:].bitcast(dt.uint8), ["q3"], [])
     for k in B4:
         dma("S", T.osc[4 * k:4 * k + 4, :], T.p3[32 * k:32 * k + 4, :], ["q3"], [])
     dma("S", T.y[:], T.ysb[:], ["ysb"], [])
-    op("A", 0.065 + 256 * 1.5 * CYC, lambda: act(T.opk[:], T.iob[:].indirect(T.offd[:, 0:16]), ACTF.Copy), ["iob", "offd"], ["opk"])
-    op("A", 0.065 + 128 * 1.5 * CYC, lambda: act(T.opn[:], T.iob[:].indirect(T.offn[:, 0:8]), ACTF.Copy), ["iob", "offn"], ["opn"])
+    AG(256, lambda: act(T.opk[:], T.iob[:].indirect(T.offd[:, 0:16]), ACTF.Copy), ["iob", "offd"], ["opk"])
+    AG(128, lambda: act(T.opn[:], T.iob[:].indirect(T.offn[:, 0:8]), ACTF.Copy), ["iob", "offn"], ["opn"])
     dma("S", T["op"][:, 0:256], T.opk[0:128:16, :], ["opk"], [])
     dma("S", T["op"][:, 256:384], T.opn[0:128:16, :], ["opn"], [])
     dma("S", T.uc[:], T.u3[:].bitcast(dt.uint8), ["u3"], [])
@@ -298,33 +312,79 @@ def rank_program(g, core, T, topo):
     plan_and_emit(g, T, ops, queue, csem)
 
 
-def plan_and_emit(g, T, ops, queue, csem):
+TRIES, FOUND = 700, {}
+ASSUMED = [(1.0, 0.07, 0.0), (0.8, 0.07, 0.0), (1.0, 0.2, 0.0), (1.2, 0.07, 1.0), (0.8, 0.07, 2.0), (1.0, 0.03, 0.0)]
+
+
+def find_order(ops):
     n = len(ops)
+    unit, cost, extra, hard = [o["u"] for o in ops], [o["cost"] for o in ops], [o["extra"] for o in ops], [sorted(o["hard"]) for o in ops]
+    need = [len(o["hard"] | o["order"]) for o in ops]
     succ = [[] for _ in range(n)]
     for o in ops:
         for d in o["hard"] | o["order"]:
             succ[d].append(o["k"])
     tail = [0.0] * n
     for k in range(n - 1, -1, -1):
-        tail[k] = ops[k]["cost"] + ops[k]["extra"] + max([tail[s] + WAKE for s in succ[k]] + [0.0])
-    free, end, seq = {}, {}, []
-    left = [len(o["hard"] | o["order"]) for o in ops]
-    ready = {k for k in range(n) if left[k] == 0}
-    while ready:
-        est = {k: max([free.get(ops[k]["u"], 0.0)] + [end[d] + WAKE for d in ops[k]["hard"]]) for k in ready}
-        lo = min(est.values())
-        k = max((k for k in ready if est[k] <= lo + 0.1), key=lambda k: (tail[k], -k))
-        o = ops[k]
-        free[o["u"]] = est[k] + o["cost"]
-        end[k] = est[k] + o["cost"] + o["extra"]
-        seq.append(k)
-        ready.discard(k)
-        for s in succ[k]:
-            left[s] -= 1
-            if left[s] == 0:
-                ready.add(s)
+        tail[k] = cost[k] + extra[k] + max([tail[s] + WAKE for s in succ[k]] + [0.0])
+
+    def plan(key):
+        left, free, end, seq = list(need), {u: 0.0 for u in unit}, [0.0] * n, []
+        ready = {k: 0.0 for k in range(n) if left[k] == 0}
+        while ready:
+            est = [(max(t, free[unit[k]]), k) for k, t in ready.items()]
+            lo = min(est)[0] + 0.06
+            t, k = max((e for e in est if e[0] <= lo), key=lambda e: (key[e[1]], -e[1]))
+            free[unit[k]] = t + cost[k]
+            end[k] = t + cost[k] + extra[k]
+            seq.append(k)
+            del ready[k]
+            for s in succ[k]:
+                left[s] -= 1
+                if left[s] == 0:
+                    ready[s] = max([end[d] + WAKE for d in hard[s]] + [0.0])
+        return seq
+
+    def ends(seq):
+        total = 0.0
+        for f, wake, late in ASSUMED:
+            free, end = {u: 0.0 for u in unit}, [0.0] * n
+            for k in seq:
+                u = unit[k]
+                t = 0.0 if u == "N" else free[u]
+                for d in hard[k]:
+                    if end[d] + wake > t:
+                        t = end[d] + wake
+                t += late + cost[k] if u == "N" else cost[k] * f if u in "VAP" else cost[k]
+                free[u] = t
+                end[k] = t + extra[k]
+            total += max(end)
+        return total
+
+    state = [12345]
+
+    def rnd(m):
+        state[0] = (state[0] * 1103515245 + 12345) % 2147483648
+        return (state[0] >> 8) % m
+    key = tail
+    best = plan(key)
+    least = ends(best)
+    for i in range(TRIES):
+        trial = list(key)
+        for _ in range(n if i < 40 else (2, 5, 12)[rnd(3)]):
+            trial[_ if i < 40 else rnd(n)] += (rnd(1000) / 1000.0) * 0.4 if i < 40 else (rnd(1000) + rnd(1000) - 1000) / 700.0
+        seq = plan(trial)
+        e = ends(seq)
+        if e < least:
+            best, least, key = seq, e, trial
+    return best
+
+
+def plan_and_emit(g, T, ops, queue, csem):
+    if len(ops) not in FOUND:
+        FOUND[len(ops)] = find_order(ops)
     count, clock, after = {}, {}, {}
-    for i, k in enumerate(seq):
+    for i, k in enumerate(FOUND[len(ops)]):
         o = ops[k]
         known = clock.setdefault(o["u"], {})
         need = {}

from concourse.mybir import dt, AluOpType, ActivationFunctionType

ALU = AluOpType
ACTF = ActivationFunctionType
STEP = [1, 2, 4]
BIG = 1.0e29
ON_SCALAR = (1, 2, 3, 4)
TS, XS, RS, VS = "AAAA", "AAVV", "AAVV", "AAVV"

SCRATCH = {
    "xin": ("sbuf", [128, 1024], "bfloat16"), "uin": ("sbuf", [128, 512], "bfloat16"), "vin": ("sbuf", [128, 512], "bfloat16"),
    "eh": ("sbuf", [128, 2048], "bfloat16"), "full": ("sbuf", [128, 512], "bfloat16"), "ioe": ("sbuf", [128, 512], "float32"),
    "iob": ("sbuf", [128, 256], "bfloat16"), "dist": ("sbuf", [128, 512], "float32"),
    "seg": ("sbuf", [128, 256], "float32"), "top": ("sbuf", [128, 256], "float32"), "ones": ("sbuf", [128, 256], "bfloat16"),
    "ib": ("sbuf", [128, 16], "int32"), "fb": ("sbuf", [128, 8], "float32"), "iw": ("sbuf", [128, 8], "int32"), "base": ("sbuf", [128, 1], "float32"),
    "dupl": ("sbuf", [128, 4], "uint16"), "seld": ("sbuf", [128, 2], "uint16"), "seln": ("sbuf", [128, 2], "uint16"),
    "st": ("sbuf", [128, 256], "float32"), "rd": ("sbuf", [128, 264], "float32"),
    "qd": ("sbuf", [128, 256], "bfloat16"), "cd": ("sbuf", [128, 256], "bfloat16"),
    "kc": ("sbuf", [128, 32], "bfloat16"), "kt": ("sbuf", [128, 32], "bfloat16"),
    "kd": ("sbuf", [128, 64], "bfloat16"), "ko": ("sbuf", [128, 64], "bfloat16"),
    "offd": ("sbuf", [128, 16], "uint16"), "offn": ("sbuf", [128, 16], "uint16"),
    "rb": ("sbuf", [128, 8 * 264], "float32"),
    "db0": ("sbuf", [128, 256], "float32"), "db1": ("sbuf", [128, 256], "float32"),
    "neb": ("sbuf", [128, 2048], "bfloat16"), "sgb": ("sbuf", [128, 2048], "bfloat16"), "cb": ("sbuf", [128, 2048], "bfloat16"),
    "junk": ("sbuf", [128, 256], "bfloat16"), "n0": ("sbuf", [128, 1], "float32"),
    "jn": ("sbuf", [128, 8], "float32"), "jm": ("sbuf", [128, 8], "float32"), "more": ("sbuf", [128, 8], "float32"),
    "less": ("sbuf", [128, 8], "float32"), "part": ("sbuf", [128, 8], "float32"), "held": ("sbuf", [128, 8], "float32"),
    "nb": ("sbuf", [128, 32], "float32"), "nt": ("sbuf", [128, 32], "float32"),
    "nd": ("sbuf", [128, 64], "bfloat16"), "ngo": ("sbuf", [128, 64], "bfloat16"),
    "du": ("sbuf", [128, 512], "bfloat16"), "tp": ("sbuf", [128, 1024], "bfloat16"), "tr": ("sbuf", [128, 1024], "bfloat16"),
    "zt": ("sbuf", [128, 1024], "bfloat16"), "xt": ("sbuf", [128, 1024], "bfloat16"), "vt": ("sbuf", [128, 512], "bfloat16"),
    "opk": ("sbuf", [128, 256], "float32"), "opn": ("sbuf", [128, 128], "float32"), "ysb": ("sbuf", [128, 256], "float32"),
    "pd": ("psum", [128, 2048], "float32"), "pr": ("psum", [128, 2048], "float32"),
}


def _pair(name, plane, n):
    SCRATCH[name] = ("sbuf", [128, n], "float8_e4m3fn_x4")
    SCRATCH[plane] = ("sbuf", [128, n], "uint8")


_pair("wq", "wp", 512)
_pair("ehq", "ehp", 512)
_pair("vcq", "vcp", 128)
for _r in range(4):
    _pair("q%d" % _r, "p%d" % _r, 256)
    _pair("u%d" % _r, "s%d" % _r, 128)
for _r in range(3):
    _pair("zq%d" % _r, "zp%d" % _r, 256)
    _pair("xl%d" % _r, "xs%d" % _r, 256)
    SCRATCH["lo%d" % _r] = ("sbuf", [128, 8], "uint16")

SEMAPHORES = ["sv", "sa", "sp", "sg"] + ["%s%d" % (n, r) for n in ("arr", "sent", "lst", "lsent") for r in range(3)] + ["d%d" % k for k in range(24)]

CYC = 0.00083 * 1.25
WAKE = 0.07


def rank_program(g, core, T, topo):
    rank = T.rank_of(core)
    if rank is None:
        return
    ops = []
    last_w, readers = {}, {}
    queue = {"V": g.vector, "A": g.scalar, "P": g.tensor, "G": g, "S": g.sync, "AD": g.scalar}
    csem = {"V": "sv", "A": "sa", "P": "sp", "G": "sg"}
    ndma = [0]

    def op(eng, cost, fn, reads=(), writes=(), sem=None, inc=1, extra=0.0):
        k = len(ops)
        hard, order = set(), set()
        for b in reads:
            if b in last_w:
                hard.add(last_w[b])
        for b in writes:
            for d in ([last_w[b]] if b in last_w else []) + readers.get(b, []):
                if eng == "P" and ops[d]["eng"] == "P" and b[:2] in ("PD", "PR"):
                    order.add(d)
                else:
                    hard.add(d)
        for b in reads:
            readers.setdefault(b, []).append(k)
        for b in writes:
            last_w[b] = k
            readers[b] = []
        ops.append({"k": k, "eng": eng, "u": "A" if eng == "AD" else eng, "cost": cost, "extra": extra, "fn": fn,
                    "hard": hard - {k}, "order": order - {k}, "sem": sem, "inc": inc, "w": list(writes)})

    def V(n, fn, reads, writes, cyc=1.0):
        op("V", max(64, n * cyc) * CYC, fn, reads, writes)

    def GA(n, fn, reads, writes):
        op("V", 0.05 + n * 1.5 * CYC, fn, reads, writes)

    def A(n, fn, reads, writes, fix=0.06):
        op("A", fix + n * CYC, fn, reads, writes)

    def AG(n, fn, reads, writes):
        op("A", 0.065 + n * 1.5 * CYC, fn, reads, writes)

    def bank(b, n=256):
        return T[b[0]][:, 512 * b[1]:512 * b[1] + n], b[0].upper() + "%d" % b[1]

    def mm(b, lhs, rhs, n, start, stop, reads):
        out, name = bank(b, n)
        op("P", (n + 16) * CYC, lambda: g.tensor.matmul_mx(out, lhs[0], lhs[1], rhs[0], rhs[1], start, stop), reads, [name])

    def dma(eng, out, in_, reads, writes, lat=2.2):
        s = "d%d" % ndma[0]
        ndma[0] += 1
        op(eng, 0.08, lambda: queue[eng].dma_start(out, in_), reads, writes, sem=s, inc=16, extra=lat)

    def quant(q, p, t, n, reads, writes):
        op("V", 0.012 + 0.00022 * 4 * n * 1.25, lambda: g.vector.quantize_mx(q, p, t), reads, writes)

    tt, ts, tc = g.vector.tensor_tensor, g.vector.tensor_scalar, g.vector.tensor_copy
    scan, act = g.vector.tensor_tensor_scan, g.scalar.activation
    B4 = range(4)

    def copy(e, o, i, n, reads, writes, scale=1.0):
        if e == "A":
            A(n, lambda: act(o, i, ACTF.Copy, scale=scale), reads, writes)
        elif scale == 1.0:
            V(n, lambda: tc(o, i), reads, writes)
        else:
            V(n, lambda: ts(o, i, scale, None, ALU.mult), reads, writes)

    dma("S", T.xin[:], T.x[:], [], ["xin"])
    dma("AD", T.uin[:], T.u[:], [], ["uin"])
    dma("S", T.wq[:].bitcast(dt.uint8), T.wc[:], [], ["wq"])
    dma("AD", T.wp[:], T.ws[:], [], ["wp"])
    dma("S", T.vin[:], T.v[:], [], ["vin"])

    op("G", 0.2, lambda: g.iota(T.iw[:, 0:4], [[0, 4]], 0, 1), [], ["iw0"])
    op("G", 1.2, lambda: g.iota(T.ioe[:], [[1, 512]], 0, -4, allow_small_or_imprecise_dtypes=True), [], ["ioe"])
    V(256, lambda: g.vector.memset(T.full[:], 32.0), [], ["full"])
    op("G", 1.3, lambda: g.affine_select(T.eh[:, 1536:2048], T.full[:], [[-1, 512]], ALU.is_equal, 0.0, 3, 4), ["full"], ["eh3"])
    op("G", 0.2, lambda: g.iota(T.iw[:, 4:8], [[16, 2], [0, 2]], 0, 0), [], ["iw1"])
    op("G", 0.7, lambda: g.iota(T.iob[:], [[1, 256]], 0, 0, allow_small_or_imprecise_dtypes=True), [], ["iob"])
    A(512, lambda: act(T.dist[:], T.ioe[:], ACTF.Abs, bias=-2.0), ["ioe"], ["dist"])
    A(512, lambda: act(T.eh[:, 1024:1536], T.dist[:], ACTF.Relu, bias=32.0, scale=-32.0), ["dist"], ["eh2"])
    for b in (0, 1):
        V(512, lambda b=b: ts(T.eh[:, 512 * b:512 * b + 512], T.ioe[:], float(b), 32.0, ALU.is_equal, ALU.mult), ["ioe"], ["eh%d" % b])
    quant(T.ehq[:], T.ehp[:], T.eh[:], 512, ["eh%d" % b for b in B4], ["ehq"])

    def col(k):
        return T.ib[:, k:k + 1]

    def fcol(k):
        return T.fb[:, k:k + 1]

    def bit(k, s1, o1, s2=None, o2=None):
        if o2 is None:
            V(1, lambda: ts(col(k), T.iw[:, 0:1], s1, None, o1), ["iw0"], ["ib%d" % k])
        else:
            V(1, lambda: ts(col(k), T.iw[:, 0:1], s1, s2, o1, o2), ["iw0"], ["ib%d" % k])
    bit(0, 15, ALU.bitwise_and)
    bit(1, 1, ALU.bitwise_and)
    bit(2, 4, ALU.logical_shift_right, 1, ALU.bitwise_and)
    bit(3, 7, ALU.bitwise_and, 1, ALU.logical_shift_right)
    bit(4, 5, ALU.logical_shift_right)
    bit(5, 4, ALU.logical_shift_right)
    V(1, lambda: tc(fcol(0), col(0)), ["ib0"], ["fb0"])
    V(1, lambda: ts(T.dupl[:], T.iw[:, 4:8], fcol(0), None, ALU.add), ["fb0", "iw1"], ["dupl"])
    V(1, lambda: tt(fcol(1), col(0), col(2), ALU.add), ["ib0", "ib2"], ["fb1"])
    V(1, lambda: ts(T.seld[:, 0:1], col(1), 31.0, fcol(1), ALU.mult, ALU.add), ["ib1", "fb1"], ["seld"])
    V(1, lambda: tc(fcol(2), col(5)), ["ib5"], ["fb2"])
    V(1, lambda: ts(T.base[:], col(5), 16.0, 15.0, ALU.mult, ALU.add), ["ib5"], ["base"])
    V(1, lambda: tt(col(7), col(3), col(4), ALU.subtract), ["ib3", "ib4"], ["ib7"])
    V(1, lambda: ts(col(8), col(7), 3, None, ALU.bitwise_and), ["ib7"], ["ib8"])
    V(1, lambda: ts(fcol(3), col(8), 8.0, fcol(2), ALU.mult, ALU.add), ["ib8", "fb2"], ["fb3"])
    V(1, lambda: ts(T.seln[:, 0:1], col(1), 32.0, fcol(3), ALU.mult, ALU.add), ["ib1", "fb3"], ["seln"])
    A(256, lambda: act(T.top[:], T.ioe[:, 0:256], ACTF.Identity, bias=BIG, scale=0.0), ["ioe"], ["top"])
    A(256, lambda: act(T.seg[:], T.ioe[:, 0:256], ACTF.Identity, bias=BIG, scale=0.0), ["ioe"], ["seg0"])
    A(16, lambda: act(T.seg[:, 0:256:16], T.ioe[:, 0:16], ACTF.Identity, bias=-BIG, scale=0.0), ["ioe", "seg0"], ["seg0"])
    A(256, lambda: act(T.ones[:], T.ioe[:, 0:256], ACTF.Identity, bias=1.0, scale=0.0), ["ioe"], ["ones"])
    V(8, lambda: g.vector.memset(T.rb[:, 0:8 * 264:264], -BIG), [], ["rbi"])
    V(1, lambda: g.vector.memset(T.rd[:, 0:1], 0.0), [], ["rd0"])
    V(16, lambda: g.vector.memset(T.kc[:], 0.0), [], ["kc"])

    def W(name, b):
        return (T[name + "q"][:, 128 * b:128 * b + 128], T[name + "p"][:, 128 * b:128 * b + 128])

    quant(T.q0[:], T.p0[:], T.xin[:], 256, ["xin"], ["q0"])
    quant(T.u0[:], T.s0[:], T.uin[:], 128, ["uin"], ["u0"])

    def unpack(q, p, to, at, how, scale):
        for b in B4:
            mm((at, b), W("eh", b), (T[q][:], T[p][:]), 256, True, True, ["ehq", q])
        for b in B4:
            i, bn = bank((at, b))
            copy(how[b], T[to][:, 256 * b:256 * b + 256], i, 256, [], ["%s%d" % (to, b), bn], scale)

    unpack("q0", "p0", "tp", "pr", TS, 0.015625)
    for r, h in enumerate(STEP):
        qn, un, q2, p2, u2, s2 = "q%d" % r, "u%d" % r, "q%d" % (r + 1), "p%d" % (r + 1), "u%d" % (r + 1), "s%d" % (r + 1)
        Q, U = (T[qn][:], T["p%d" % r][:]), (T[un][:], T["s%d" % r][:])
        Z = (T["zq%d" % r][:], T["zp%d" % r][:])
        dst = T.cores[(rank + h) % len(T.cores)]
        rid, pid, _ = topo.addr(dst)
        m, ne = topo.mask(core, dst), len(topo.engines(core, dst))

        def send(cost, lat, moves, reads, writes, arr, sent, rid=rid, pid=pid, m=m, ne=ne):
            def go():
                for o, i in moves:
                    g.remote_dma(o, i, T.sem[arr], T.sem[sent], pid, rid, m)
            op("G", cost, go, reads, [sent], sem=sent, inc=len(moves) * ne)
            op("N", lat, None, [sent], writes, sem=arr, inc=len(moves) * ne)

        mm(("pd", 0), U, Q, 256, True, True, [qn, un])
        mm(("pd", 1), U, Q, 256, True, True, [qn, un])
        for b in B4:
            at = ("pd", 2 + b % 2) if r == 0 else ("pr", b)
            mm(at, W("eh", b), U, 128, True, True, ["ehq", un])
            i, bn = bank(at, 128)
            copy("A", T.du[:, 128 * b:128 * b + 128], i, 128, [], ["du%d" % b, bn], 0.015625)
        for b in B4:
            mm(("pr", b), W("eh", b), Q, 256, True, False, ["ehq", qn])
        V(256, lambda: g.vector.transpose(T.st[:], T.pd[:, 0:256]), [], ["st", "PD0"])
        V(256, lambda: scan(T.rd[:, 1:257], T.seg[:], T.st[:], 0.0, ALU.min, ALU.max), ["seg0", "st"], ["rd"])
        V(256, lambda: tt(T.qd[:], T.rd[:, 0:256], T.st[:], ALU.is_ge), ["rd", "rd0", "st"], ["qd"], 2.0)
        V(256, lambda: scan(T.cd[:], T.qd[:], T.qd[:], 0.0, ALU.mult, ALU.add), ["qd"], ["cd"], 0.5)
        V(16, lambda: ts(T.kc[:, 0:16], T.cd[:, 15:256:16], 15.0, None, ALU.min), ["cd"], ["kc"])
        V(32, lambda: g.vector.transpose(T.kt[:], T.kc[:]), ["kc"], ["kt"])
        GA(64, lambda: tc(T.kd[:], T.kt[:, 0:32].indirect(T.dupl[:, 0:4])), ["kt", "dupl"], ["kd"])
        V(64, lambda: g.vector.transpose(T.ko[:], T.kd[:]), ["kd"], ["ko"])
        GA(16, lambda: ts(T.offd[:], T.ko[:, 0:64].indirect(T.seld[:, 0:1]), -1.0, T.base[:], ALU.mult, ALU.add), ["ko", "seld", "base"], ["offd"])
        for b in B4:
            GA(256, lambda b=b: tt(T.zt[:, b:1024:4], T.du[:, 128 * b:128 * b + 128].indirect(T.offd[:, 0:16]), T.tp[:, 256 * b:256 * b + 256], ALU.add),
               ["du%d" % b, "offd", "tp%d" % b], ["zt%d" % b])
        quant(Z[0], Z[1], T.zt[:], 256, ["zt%d" % b for b in B4], ["zq%d" % r])
        for b in B4:
            mm(("pr", b), W("w", b), Z, 256, False, True, ["wq", "wp", "zq%d" % r])
        for b in B4:
            i, bn = bank(("pr", b))
            copy(XS[b], T.xt[:, b:1024:4], i, 256, [], ["xt%d" % b, bn], 0.03125)
        quant(T[q2][:], T[p2][:], T.xt[:], 256, ["xt%d" % b for b in B4], [q2])
        send(1.0, 3.0, [(T["xl%d" % r][:].bitcast(dt.uint8), T[q2][:].bitcast(dt.uint8)), (T["xs%d" % r][:], T[p2][:])],
             [q2], ["xl%d" % r], "arr%d" % r, "sent%d" % r)
        for k in range(8):
            o, kk = 264 * k, slice(k, k + 1)
            run, v, w = T.rb[:, o + 1:o + 257], T.rb[:, o + 256:o + 257], T.rb[:, o - 8:o - 7]
            if k == 0:
                V(256, lambda run=run: scan(run, T.top[:], T.pd[:, 0:256], -2.0 * BIG, ALU.min, ALU.max), ["top"], ["rb0", "PD0"])
                A(256, lambda run=run, v=v: act(T.junk[:], run, ACTF.Sign, bias=v, scale=-1.0, accum_out=T.n0[:]), ["rb0"], ["junk", "n0"], 0.1)
                A(1, lambda: act(T.nb[:, 0:1], T.n0[:], ACTF.Identity, bias=-256.0, scale=2.0), ["n0"], ["nb0"])
                continue
            dk, ok = "db%d" % (k % 2), "db%d" % ((k - 1) % 2)
            out, old, shifted = T[dk][:], T[ok][:], T.rb[:, o - 264:o - 8]
            if k == 1:
                V(256, lambda out=out, x=shifted: scan(out, x, T.pd[:, 0:256], -2.0 * BIG, ALU.max, ALU.min), ["rb0", "rbi"], [dk, "PD0"])
            else:
                V(256, lambda out=out, x=shifted, old=old: scan(out, x, old, -2.0 * BIG, ALU.max, ALU.min), ["rb%d" % (k - 1), "rbi", ok], [dk])
            V(256, lambda out=out, run=run: scan(run, out, out, -2.0 * BIG, ALU.max, ALU.max), [dk, "rbi"], ["rb%d" % k])
            e, c, f = [T[x][:, 256 * k:256 * k + 256] for x in ("neb", "cb", "sgb")]
            if k in ON_SCALAR:
                A(256, lambda f=f, v=v, kk=kk: act(f, T.pd[:, 512:768], ACTF.Sign, bias=v, scale=-1.0, accum_out=T.less[:, kk]),
                  ["rb%d" % k], ["sgb%d" % k, "less%d" % k, "PD1"], 0.08)
                A(256, lambda f=f, e=e, kk=kk: act(e, f, ACTF.Abs, accum_out=T.more[:, kk]), ["sgb%d" % k], ["neb%d" % k, "more%d" % k], 0.08)
                A(1, lambda k=k, kk=kk: act(T.part[:, kk], T.less[:, kk], ACTF.Identity, bias=k + 0.5, scale=0.5), ["less%d" % k], ["part%d" % k])
                A(1, lambda kk=kk: act(T.held[:, kk], T.more[:, kk], ACTF.Identity, bias=T.part[:, kk], scale=-0.5),
                  ["more%d" % k, "part%d" % k], ["held%d" % k])
                first, half, need = 0.0, T.held[:, kk], []
                if k < 7 and k + 1 not in ON_SCALAR:
                    A(1, lambda kk=kk: act(T.jm[:, kk], T.held[:, kk], ACTF.Identity, bias=0.5), ["held%d" % k], ["jm%d" % k])
            else:
                V(256, lambda e=e, v=v: ts(e, T.pd[:, 0:256], v, None, ALU.not_equal), ["rb%d" % k], ["neb%d" % k, "PD0"])
                V(1, lambda v=v, w=w, k=k, kk=kk: ts(T.jn[:, kk], v, w, T.jm[:, k - 1:k], ALU.is_equal, ALU.mult),
                  ["rb%d" % k, "rb%d" % (k - 1), "jm%d" % (k - 1)], ["jn%d" % k])
                if k < 7 and k + 1 not in ON_SCALAR:
                    A(1, lambda kk=kk: act(T.jm[:, kk], T.jn[:, kk], ACTF.Identity, bias=1.0), ["jn%d" % k], ["jm%d" % k])
                first, half, need = T.jn[:, kk], 0.5, ["jn%d" % k]
            V(256, lambda e=e, c=c, first=first: scan(c, e, T.ones[:], first, ALU.add, ALU.subtract), ["neb%d" % k, "ones"] + need, ["cb%d" % k], 0.5)
            A(256, lambda c=c, kk=kk, half=half: act(T.junk[:], c, ACTF.Sign, bias=half, accum_out=T.nb[:, kk]),
              ["cb%d" % k] + ([] if need else ["held%d" % k]), ["junk", "nb%d" % k], 0.1)
        NB = ["nb%d" % k for k in range(8)]
        for q in B4:
            copy("VA"[q % 2], T.nb[32 * q:32 * q + 32, 8:16], T.nb[32 * ((q + 1) % 4):32 * ((q + 1) % 4) + 32, 0:8], 8, NB, ["nx%d" % q])
        NX = NB + ["nx%d" % q for q in B4]
        copy("V", T.nb[0:64, 16:32], T.nb[64:128, 0:16], 16, NX, ["ny0"])
        copy("A", T.nb[64:128, 16:32], T.nb[0:64, 0:16], 16, NX, ["ny1"])
        V(32, lambda: g.vector.transpose(T.nt[:], T.nb[:]), NX + ["ny0", "ny1"], ["nt"])
        GA(64, lambda: tc(T.nd[:], T.nt[:, 0:32].indirect(T.dupl[:, 0:4])), ["nt", "dupl"], ["nd"])
        V(64, lambda: g.vector.transpose(T.ngo[:], T.nd[:]), ["nd"], ["ngo"])
        GA(16, lambda: ts(T.offn[:], T.ngo[:, 0:64].indirect(T.seln[:, 0:1]), 0.5, 128.0, ALU.mult, ALU.add), ["ngo", "seln"], ["offn"])
        send(0.5, 1.5, [(T["lo%d" % r][:], T.offn[:, 0:8])], ["offn"], ["lo%d" % r], "lst%d" % r, "lsent%d" % r)
        unpack("xl%d" % r, "xs%d" % r, "tr", "pr", RS, 0.03125)
        if r < 2:
            unpack(q2, p2, "tp", "pd", TS, 0.015625)
        for b in B4:
            o, i = T.vt[:, b:512:4], T.tr[:, 256 * b:256 * b + 256].indirect(T["lo%d" % r][:, 0:8])
            if VS[b] == "A":
                AG(128, lambda o=o, i=i: act(o, i, ACTF.Copy), ["tr%d" % b, "lo%d" % r], ["vt%d" % b])
            else:
                GA(128, lambda o=o, i=i: tc(o, i), ["tr%d" % b, "lo%d" % r], ["vt%d" % b])
        quant(T[u2][:], T[s2][:], T.vt[:], 128, ["vt%d" % b for b in B4], [u2])
        if r == 0:
            quant(T.vcq[:], T.vcp[:], T.vin[:], 128, ["vin"], ["vcq"])
    mm(("pd", 2), (T.vcq[:], T.vcp[:]), (T.q3[:], T.p3[:]), 256, True, True, ["vcq", "q3"])
    copy("A", T.ysb[:], bank(("pd", 2))[0], 256, [], ["ysb", "PD2"])
    dma("S", T.oc[:], T.q3[:].bitcast(dt.uint8), ["q3"], [])
    for k in B4:
        dma("S", T.osc[4 * k:4 * k + 4, :], T.p3[32 * k:32 * k + 4, :], ["q3"], [])
    dma("S", T.y[:], T.ysb[:], ["ysb"], [])
    AG(256, lambda: act(T.opk[:], T.iob[:].indirect(T.offd[:, 0:16]), ACTF.Copy), ["iob", "offd"], ["opk"])
    AG(128, lambda: act(T.opn[:], T.iob[:].indirect(T.offn[:, 0:8]), ACTF.Copy), ["iob", "offn"], ["opn"])
    dma("S", T["op"][:, 0:256], T.opk[0:128:16, :], ["opk"], [])
    dma("S", T["op"][:, 256:384], T.opn[0:128:16, :], ["opn"], [])
    dma("S", T.uc[:], T.u3[:].bitcast(dt.uint8), ["u3"], [])
    for k in B4:
        dma("AD" if k % 2 else "S", T.usc[4 * k:4 * k + 4, :], T.s3[32 * k:32 * k + 4, :], ["u3"], [])
    plan_and_emit(g, T, ops, queue, csem)


TRIES, FOUND = 700, {}
ASSUMED = [(1.0, 0.07, 0.0), (0.8, 0.07, 0.0), (1.0, 0.2, 0.0), (1.2, 0.07, 1.0), (0.8, 0.07, 2.0), (1.0, 0.03, 0.0)]


def find_order(ops):
    n = len(ops)
    unit, cost, extra, hard = [o["u"] for o in ops], [o["cost"] for o in ops], [o["extra"] for o in ops], [sorted(o["hard"]) for o in ops]
    need = [len(o["hard"] | o["order"]) for o in ops]
    succ = [[] for _ in range(n)]
    for o in ops:
        for d in o["hard"] | o["order"]:
            succ[d].append(o["k"])
    tail = [0.0] * n
    for k in range(n - 1, -1, -1):
        tail[k] = cost[k] + extra[k] + max([tail[s] + WAKE for s in succ[k]] + [0.0])

    def plan(key):
        left, free, end, seq = list(need), {u: 0.0 for u in unit}, [0.0] * n, []
        ready = {k: 0.0 for k in range(n) if left[k] == 0}
        while ready:
            est = [(max(t, free[unit[k]]), k) for k, t in ready.items()]
            lo = min(est)[0] + 0.06
            t, k = max((e for e in est if e[0] <= lo), key=lambda e: (key[e[1]], -e[1]))
            free[unit[k]] = t + cost[k]
            end[k] = t + cost[k] + extra[k]
            seq.append(k)
            del ready[k]
            for s in succ[k]:
                left[s] -= 1
                if left[s] == 0:
                    ready[s] = max([end[d] + WAKE for d in hard[s]] + [0.0])
        return seq

    def ends(seq):
        total = 0.0
        for f, wake, late in ASSUMED:
            free, end = {u: 0.0 for u in unit}, [0.0] * n
            for k in seq:
                u = unit[k]
                t = 0.0 if u == "N" else free[u]
                for d in hard[k]:
                    if end[d] + wake > t:
                        t = end[d] + wake
                t += late + cost[k] if u == "N" else cost[k] * f if u in "VAP" else cost[k]
                free[u] = t
                end[k] = t + extra[k]
            total += max(end)
        return total

    state = [12345]

    def rnd(m):
        state[0] = (state[0] * 1103515245 + 12345) % 2147483648
        return (state[0] >> 8) % m
    key = tail
    best = plan(key)
    least = ends(best)
    for i in range(TRIES):
        trial = list(key)
        for _ in range(n if i < 40 else (2, 5, 12)[rnd(3)]):
            trial[_ if i < 40 else rnd(n)] += (rnd(1000) / 1000.0) * 0.4 if i < 40 else (rnd(1000) + rnd(1000) - 1000) / 700.0
        seq = plan(trial)
        e = ends(seq)
        if e < least:
            best, least, key = seq, e, trial
    return best


def plan_and_emit(g, T, ops, queue, csem):
    if len(ops) not in FOUND:
        FOUND[len(ops)] = find_order(ops)
    count, clock, after = {}, {}, {}
    for i, k in enumerate(FOUND[len(ops)]):
        o = ops[k]
        known = clock.setdefault(o["u"], {})
        need = {}
        for d in sorted(o["hard"], key=lambda d: -after[d][2]):
            s, v, _, seen = after[d]
            if known.get(s, 0) >= v:
                continue
            need[s] = max(need.get(s, 0), v)
            for a, b in seen.items():
                known[a] = max(known.get(a, 0), b)
            known[s] = max(known.get(s, 0), v)
        if o["fn"] is not None:
            for s, v in need.items():
                queue[o["eng"]].wait_ge(T.sem[s], v)
        s = o["sem"] or csem[o["eng"]]
        count[s] = count.get(s, 0) + o["inc"]
        if o["fn"] is not None:
            c = o["fn"]()
            if c is not None:
                c.then_inc(T.sem[s], o["inc"])
        after[k] = (s, count[s], i, dict(known) if o["fn"] is not None else {})
    for s, v in count.items():
        if clock["G"].get(s, 0) < v:
            g.wait_ge(T.sem[s], v)
